import numpy as np
import ml_dtypes


def mxq(x, axis, fmt="e4m3"):
    dtype, down = {"e4m3": (ml_dtypes.float8_e4m3fn, 7), "e5m2": (ml_dtypes.float8_e5m2, 14)}[fmt]
    v = np.moveaxis(np.asarray(x, np.float32).astype(ml_dtypes.bfloat16).astype(np.float64), axis, -1)
    blocks = v.reshape(v.shape[:-1] + (-1, 32))
    amax = np.abs(blocks).max(-1, keepdims=True)
    byte = np.maximum(np.where(amax > 0, np.frexp(amax)[1] - 1 + 127, 0) - down, 1)
    scale = np.exp2(byte - 127.0)
    codes = (blocks / scale).astype(np.float32).astype(dtype).astype(np.float64)
    return np.moveaxis((codes * scale).reshape(v.shape), -1, axis)


WIDE = False


def mx_kscale(k):
    if not WIDE:
        return np.ones(k)
    levels = np.array([10, -10, 5, -5, 0])
    if k % 512:
        return np.exp2(np.random.permutation(np.resize(levels, k // 32))).repeat(32)
    a = np.empty((k // 512, 16))
    for p in range(k // 512):
        a[p, :8] = np.random.permutation(np.resize(levels, 8))
        for g in range(8):
            far = levels[np.abs(levels - a[p, g]) >= 10]
            a[p, g + 8] = far[np.random.randint(len(far))]
    return np.exp2(a.ravel()).repeat(32)


def f64(x):
    return np.asarray(x).astype(np.float64)


def striped(idx):
    return np.tile(idx.reshape(-1, 16).T, (8, 1)).astype(np.uint16)


def unstriped(offs):
    return offs[:16].T.reshape(-1).astype(np.int64)


def pack_weight(w):
    k, n = w.shape
    w = f64(np.asarray(w, np.float32).astype(ml_dtypes.bfloat16)).reshape(k // 32, 32, n)
    amax = np.abs(w).max(1)
    byte = np.clip(np.where(amax > 0, np.frexp(amax)[1] - 1 + 127 - 7, 1), 1, 254)
    scaled = (w * np.exp2(127.0 - byte)[:, None, :]).reshape(k, n).astype(np.float32)
    words = np.ascontiguousarray(scaled.reshape(k // 512, 128, 4, n).transpose(0, 1, 3, 2)).astype(ml_dtypes.float8_e4m3fn).view(np.uint8)
    return words, np.ascontiguousarray(byte.astype(np.uint8).reshape(k // 512, 16, n))


def unpack_weight(words, scales):
    g, p, n, _ = words.shape
    vals = np.ascontiguousarray(words).view(ml_dtypes.float8_e4m3fn).astype(np.float64) * np.repeat(np.exp2(scales.astype(np.float64) - 127.0), 8, axis=1)[..., None]
    return vals.transpose(0, 1, 3, 2).reshape(g * 512, n)


def sigmoid(v):
    return 1.0 / (1.0 + np.exp(-np.maximum(v, -700.0)))


K, T, S, V, D = 1024, 2048, 512, 512, 4


def setup_inputs():
    n = np.random.standard_normal
    s = mx_kscale(K)[:, None]
    packed_xT = pack_weight(n((K, T)) * s)
    return {
        "x_words": packed_xT[0],
        "x_scales": packed_xT[1],
        "hT": (n((K, V)) / np.sqrt(K) / s).astype(np.float32),
        "goal": ((np.random.uniform(size=(V, S)) < 0.4) * 1.0).astype(np.float32),
        "offs": striped(np.random.permutation(T)[:S]),
    }


def reference(x_words, x_scales, hT, goal, offs):
    hTq = mxq(f64(hT), 0, "e4m3")
    xq = unpack_weight(x_words, x_scales)[:, unstriped(offs)]
    p = sigmoid(hTq.T @ xq)
    ee = (f64(goal) - p) ** 2
    dd = ee.reshape(len(ee), -1, D).mean(axis=2)
    gg = p * f64(goal)
    z = gg.reshape(len(gg), -1, D).sum(axis=2)
    a = p.reshape(len(p), -1, D).sum(axis=2)
    return dd - ((2.0 * z + 1.0) / (a + 4.0))

@@ -1,0 +1,163 @@
+from contextlib import ExitStack
+
+import concourse.mybir as mybir
+from concourse.masks import make_identity
+
+K, T, S, V, D = 1024, 2048, 512, 512, 4
+FLOPS = 2 * K * S * V
+
+F32 = mybir.dt.float32
+BF16 = mybir.dt.bfloat16
+I32 = mybir.dt.int32
+U32 = mybir.dt.uint32
+U16 = mybir.dt.uint16
+U8 = mybir.dt.uint8
+FP8X4 = mybir.dt.float8_e4m3fn_x4
+ACT = mybir.ActivationFunctionType
+ALU = mybir.AluOpType
+
+P = 128
+PASSES = K // (4 * P)
+BLOCKS = V // P
+RUNS = S // D
+
+
+def tile_picked_ydice_dice_p_kernel(tc, x_words, x_scales, hT, goal, offs, out):
+    nc = tc.nc
+    with ExitStack() as ctx:
+        keep = ctx.enter_context(tc.tile_pool(name="keep", bufs=1))
+        work = ctx.enter_context(tc.tile_pool(name="work", bufs=2))
+        psum = ctx.enter_context(tc.psum_pool(name="psum", bufs=1))
+
+        offsets = keep.tile([P, S // 16], U16, name="offsets")
+
+        table_words = [keep.tile([P, T], U32, name="table_words%d" % o) for o in range(PASSES)]
+        table_scales = keep.tile([P, T], U8, name="table_scales")
+        h_raw = [[keep.tile([P, 4, P], F32, name="h_raw%d_%d" % (b, o)) for o in range(PASSES)] for b in range(BLOCKS)]
+        goal_sb = [keep.tile([P, S], F32, name="goal%d" % b) for b in range(BLOCKS)]
+        ident = keep.tile([P, P], F32, name="ident")
+        make_identity(nc, ident[:])
+        nc.vector.memset(table_scales[:].bitcast(I32), 0)
+
+        def load_words(o):
+            nc.sync.dma_start(table_words[o][:].bitcast(I32), x_words[o].rearrange("p c r -> p (c r)").bitcast(I32))
+
+        def load_h(b):
+            for o in range(PASSES):
+                rows = hT[o * 4 * P:(o + 1) * 4 * P, b * P:(b + 1) * P]
+                nc.sync.dma_start(h_raw[b][o][:], rows.rearrange("(p j) t -> p j t", j=4))
+
+        def load_goal(b):
+            nc.sync.dma_start(goal_sb[b][:], goal[b * P:(b + 1) * P, :])
+
+        load_words(0)
+        nc.sync.dma_start(offsets[:], offs)
+        for q in range(4):
+            nc.sync.dma_start(table_scales[32 * q:32 * q + 4 * PASSES, :].bitcast(I32),
+                              x_scales[:, 4 * q:4 * q + 4, :].bitcast(I32))
+        load_h(0)
+        load_words(1)
+        for b in range(BLOCKS):
+            if b + 1 < BLOCKS:
+                load_h(b + 1)
+            load_goal(b)
+
+        x_codes = [keep.tile([P, S], U32, name="x_codes%d" % o, align_bytes=64) for o in range(PASSES)]
+        x_planes = keep.tile([P, S], U8, name="x_planes", align_bytes=64)
+        h_codes = [keep.tile([P, PASSES * P], U32, name="h_codes%d" % b, align_bytes=64) for b in range(BLOCKS)]
+        h_planes = [keep.tile([P, PASSES * P], U8, name="h_planes%d" % b, align_bytes=64) for b in range(BLOCKS)]
+        grouped = [keep.tile([P, PASSES, P, 4], BF16, name="grouped%d" % b, align_bytes=64) for b in range(BLOCKS)]
+
+        def cast(b, o, engine):
+            dst = grouped[b][:, o].rearrange("p (c i) j -> p c j i", i=4)
+            src = h_raw[b][o][:].rearrange("p j (c i) -> p c j i", i=4)
+            if engine == "vector":
+                nc.vector.tensor_copy(out=dst, in_=src)
+            else:
+                nc.scalar.copy(out=dst, in_=src)
+
+        def quantize(b):
+            nc.vector.quantize_mx(out=h_codes[b][:].bitcast(FP8X4), scales=h_planes[b][:],
+                                  in_=grouped[b][:].rearrange("p o t j -> p (o t j)"))
+
+        state = {}
+
+        def product(b):
+            u = psum.tile([P, S], F32, name="u", tag="u", bufs=2)
+            for o in range(PASSES):
+                cols = slice(o * P, (o + 1) * P)
+                nc.tensor.matmul_mx(out=u[:], lhsT=h_codes[b][:, cols].bitcast(FP8X4), lhsT_scale=h_planes[b][:, cols],
+                                    rhs=x_codes[o][:].bitcast(FP8X4), rhs_scale=x_planes[4 * o:P, :],
+                                    start=(o == 0), stop=(o == PASSES - 1))
+            tau = work.tile([P, 2, S // 2], F32, name="tau")
+            nc.scalar.activation(out=tau[:], in_=u[:].rearrange("p (w l) -> p l w", l=2), func=ACT.Tanh, scale=0.5)
+            state["tau", b] = tau
+
+        def run_sums(tag, bufs, values):
+            acc = psum.tile([P, P], F32, name=tag, tag=tag, bufs=bufs)
+            for d in range(D):
+                nc.tensor.matmul(out=acc[:], lhsT=values[:, d // 2, d % 2::2], rhs=ident[:], is_transpose=True,
+                                 start=(d == 0), stop=(d == D - 1))
+            return acc
+
+        def elementwise(b):
+            tau = state["tau", b]
+            g = goal_sb[b][:].rearrange("p (w l) -> p l w", l=2)
+            miss = work.tile([P, 2, S // 2], F32, name="miss")
+            both = work.tile([P, 2, S // 2], F32, name="both")
+            nc.vector.scalar_tensor_tensor(out=miss[:], in0=tau[:], scalar=-0.5, in1=g, op0=ALU.mult, op1=ALU.add)
+            nc.vector.scalar_tensor_tensor(out=both[:], in0=tau[:], scalar=1.0, in1=g, op0=ALU.add, op1=ALU.mult)
+            sum_tau = run_sums("sum_tau", 1, tau)
+            den = work.tile([P, P], F32, name="den")
+            nc.scalar.activation(out=den[:], in_=sum_tau[:], func=ACT.Copy, scale=0.5, bias=6.0)
+            squares = work.tile([P, 2, S // 2], F32, name="squares")
+            nc.scalar.activation(out=squares[:], in_=miss[:], func=ACT.Square, scale=0.5, bias=-0.25)
+            state["den", b] = den
+            state["both", b] = run_sums("sum_both", 2, both)
+            state["dd", b] = run_sums("dd", 2, squares)
+
+        def inverse(b):
+            den = state["den", b]
+            m2 = work.tile([P, 2, P // 4], F32, name="m2")
+            nc.vector.tensor_tensor(out=m2[:].rearrange("p h c -> p (h c)"), in0=den[:, 0:P // 2], in1=den[:, P // 2:P], op=ALU.mult)
+            m4 = work.tile([P, P // 4], F32, name="m4")
+            nc.vector.tensor_tensor(out=m4[:], in0=m2[:, 0], in1=m2[:, 1], op=ALU.mult)
+            r4 = work.tile([P, P // 4], F32, name="r4")
+            nc.vector.reciprocal(out=r4[:], in_=m4[:])
+            r2 = work.tile([P, 2, P // 4], F32, name="r2")
+            nc.vector.tensor_tensor(out=r2[:], in0=m2[:, ::-1, :], in1=r4[:].unsqueeze(1).to_broadcast([P, 2, P // 4]), op=ALU.mult)
+            inv = work.tile([P, 2, P // 2], F32, name="inv")
+            nc.vector.tensor_tensor(out=inv[:], in0=den[:].rearrange("p (h c) -> p h c", h=2)[:, ::-1, :],
+                                    in1=r2[:].rearrange("p h c -> p (h c)").unsqueeze(1).to_broadcast([P, 2, P // 2]), op=ALU.mult)
+            state["inv", b] = inv
+
+        def finish(b):
+            ratio = work.tile([P, P], F32, name="ratio")
+            nc.vector.scalar_tensor_tensor(out=ratio[:], in0=state["both", b][:], scalar=1.0,
+                                           in1=state["inv", b][:].rearrange("p h c -> p (h c)"), op0=ALU.add, op1=ALU.mult)
+            loss = work.tile([P, P], F32, name="loss")
+            nc.vector.tensor_tensor(out=loss[:], in0=state["dd", b][:], in1=ratio[:], op=ALU.subtract)
+            turned = psum.tile([P, P], F32, name="turned", tag="turned", bufs=1)
+            nc.tensor.transpose(turned[:], loss[:], ident[:])
+            result = work.tile([P, P], F32, name="result")
+            nc.scalar.copy(out=result[:], in_=turned[:])
+            nc.sync.dma_start(out[b * P:(b + 1) * P, :], result[:])
+
+        nc.vector.tensor_copy(x_codes[0][:], table_words[0][:].indirect(offsets[:]))
+        nc.vector.tensor_copy(x_planes[:], table_scales[:].indirect(offsets[:]))
+        cast(0, 0, "scalar")
+        cast(0, 1, "scalar")
+        quantize(0)
+        nc.vector.tensor_copy(x_codes[1][:], table_words[1][:].indirect(offsets[:]))
+        product(0)
+        for b in range(BLOCKS):
+            if b + 1 < BLOCKS:
+                cast(b + 1, 0, "scalar")
+                cast(b + 1, 1, "scalar")
+                quantize(b + 1)
+                product(b + 1)
+            if b > 0:
+                finish(b - 1)
+            elementwise(b)
+            inverse(b)
+        finish(BLOCKS - 1)

@@ -20,13 +20,15 @@ P = 128
 PASSES = K // (4 * P)
 BLOCKS = V // P
 RUNS = S // D
+L1_BLOCKS = (0, 1)
+CAST_ENGINES = [["scalar","vector"],["scalar","vector"],["scalar","vector"],["scalar","vector"]]
 
 
 def tile_picked_ydice_dice_p_kernel(tc, x_words, x_scales, hT, goal, offs, out):
     nc = tc.nc
     with ExitStack() as ctx:
         keep = ctx.enter_context(tc.tile_pool(name="keep", bufs=1))
-        work = ctx.enter_context(tc.tile_pool(name="work", bufs=2))
+        work = ctx.enter_context(tc.tile_pool(name="work", bufs=4))
         psum = ctx.enter_context(tc.psum_pool(name="psum", bufs=1))
 
         offsets = keep.tile([P, S // 16], U16, name="offsets")
@@ -36,8 +38,7 @@ def tile_picked_ydice_dice_p_kernel(tc, x_words, x_scales, hT, goal, offs, out):
         h_raw = [[keep.tile([P, 4, P], F32, name="h_raw%d_%d" % (b, o)) for o in range(PASSES)] for b in range(BLOCKS)]
         goal_sb = [keep.tile([P, S], F32, name="goal%d" % b) for b in range(BLOCKS)]
         ident = keep.tile([P, P], F32, name="ident")
-        make_identity(nc, ident[:])
-        nc.vector.memset(table_scales[:].bitcast(I32), 0)
+        nc.gpsimd.memset(table_scales[:].bitcast(I32), 0)
 
         def load_words(o):
             nc.sync.dma_start(table_words[o][:].bitcast(I32), x_words[o].rearrange("p c r -> p (c r)").bitcast(I32))
@@ -55,8 +56,9 @@ def tile_picked_ydice_dice_p_kernel(tc, x_words, x_scales, hT, goal, offs, out):
         for q in range(4):
             nc.sync.dma_start(table_scales[32 * q:32 * q + 4 * PASSES, :].bitcast(I32),
                               x_scales[:, 4 * q:4 * q + 4, :].bitcast(I32))
-        load_h(0)
+        make_identity(nc, ident[:])
         load_words(1)
+        load_h(0)
         for b in range(BLOCKS):
             if b + 1 < BLOCKS:
                 load_h(b + 1)
@@ -66,7 +68,7 @@ def tile_picked_ydice_dice_p_kernel(tc, x_words, x_scales, hT, goal, offs, out):
         x_planes = keep.tile([P, S], U8, name="x_planes", align_bytes=64)
         h_codes = [keep.tile([P, PASSES * P], U32, name="h_codes%d" % b, align_bytes=64) for b in range(BLOCKS)]
         h_planes = [keep.tile([P, PASSES * P], U8, name="h_planes%d" % b, align_bytes=64) for b in range(BLOCKS)]
-        grouped = [keep.tile([P, PASSES, P, 4], BF16, name="grouped%d" % b, align_bytes=64) for b in range(BLOCKS)]
+        grouped = {}
 
         def cast(b, o, engine):
             dst = grouped[b][:, o].rearrange("p (c i) j -> p c j i", i=4)
@@ -79,6 +81,11 @@ def tile_picked_ydice_dice_p_kernel(tc, x_words, x_scales, hT, goal, offs, out):
         def quantize(b):
             nc.vector.quantize_mx(out=h_codes[b][:].bitcast(FP8X4), scales=h_planes[b][:],
                                   in_=grouped[b][:].rearrange("p o t j -> p (o t j)"))
+
+        def quantize_pass(b, o):
+            cols = slice(o * P, (o + 1) * P)
+            nc.vector.quantize_mx(out=h_codes[b][:, cols].bitcast(FP8X4), scales=h_planes[b][:, cols],
+                                  in_=grouped[b][:, o].rearrange("p t j -> p (t j)"))
 
         state = {}
 
@@ -93,71 +100,89 @@ def tile_picked_ydice_dice_p_kernel(tc, x_words, x_scales, hT, goal, offs, out):
             nc.scalar.activation(out=tau[:], in_=u[:].rearrange("p (w l) -> p l w", l=2), func=ACT.Tanh, scale=0.5)
             state["tau", b] = tau
 
-        def run_sums(tag, bufs, values):
+        def turned_sum(tag, bufs, parts):
             acc = psum.tile([P, P], F32, name=tag, tag=tag, bufs=bufs)
-            for d in range(D):
-                nc.tensor.matmul(out=acc[:], lhsT=values[:, d // 2, d % 2::2], rhs=ident[:], is_transpose=True,
-                                 start=(d == 0), stop=(d == D - 1))
+            for n, part in enumerate(parts):
+                nc.tensor.matmul(out=acc[:], lhsT=part, rhs=ident[:], is_transpose=True,
+                                 start=(n == 0), stop=(n == len(parts) - 1))
             return acc
 
-        def elementwise(b):
-            tau = state["tau", b]
-            g = goal_sb[b][:].rearrange("p (w l) -> p l w", l=2)
-            miss = work.tile([P, 2, S // 2], F32, name="miss")
-            both = work.tile([P, 2, S // 2], F32, name="both")
-            nc.vector.scalar_tensor_tensor(out=miss[:], in0=tau[:], scalar=-0.5, in1=g, op0=ALU.mult, op1=ALU.add)
-            nc.vector.scalar_tensor_tensor(out=both[:], in0=tau[:], scalar=1.0, in1=g, op0=ALU.add, op1=ALU.mult)
-            sum_tau = run_sums("sum_tau", 1, tau)
-            den = work.tile([P, P], F32, name="den")
-            nc.scalar.activation(out=den[:], in_=sum_tau[:], func=ACT.Copy, scale=0.5, bias=6.0)
-            squares = work.tile([P, 2, S // 2], F32, name="squares")
-            nc.scalar.activation(out=squares[:], in_=miss[:], func=ACT.Square, scale=0.5, bias=-0.25)
-            state["den", b] = den
-            state["both", b] = run_sums("sum_both", 2, both)
-            state["dd", b] = run_sums("dd", 2, squares)
+        def stepped(values):
+            return [values[:, l, h::2] for l in range(2) for h in range(2)]
 
         def inverse(b):
             den = state["den", b]
-            m2 = work.tile([P, 2, P // 4], F32, name="m2")
-            nc.vector.tensor_tensor(out=m2[:].rearrange("p h c -> p (h c)"), in0=den[:, 0:P // 2], in1=den[:, P // 2:P], op=ALU.mult)
-            m4 = work.tile([P, P // 4], F32, name="m4")
-            nc.vector.tensor_tensor(out=m4[:], in0=m2[:, 0], in1=m2[:, 1], op=ALU.mult)
-            r4 = work.tile([P, P // 4], F32, name="r4")
-            nc.vector.reciprocal(out=r4[:], in_=m4[:])
-            r2 = work.tile([P, 2, P // 4], F32, name="r2")
-            nc.vector.tensor_tensor(out=r2[:], in0=m2[:, ::-1, :], in1=r4[:].unsqueeze(1).to_broadcast([P, 2, P // 4]), op=ALU.mult)
+            pairs = work.tile([P, P // 2], F32, name="pairs")
+            nc.vector.tensor_tensor(out=pairs[:], in0=den[:, 0:P // 2], in1=den[:, P // 2:P], op=ALU.mult)
+            pairs_inv = work.tile([P, P // 2], F32, name="pairs_inv")
+            nc.vector.reciprocal(out=pairs_inv[:], in_=pairs[:])
             inv = work.tile([P, 2, P // 2], F32, name="inv")
             nc.vector.tensor_tensor(out=inv[:], in0=den[:].rearrange("p (h c) -> p h c", h=2)[:, ::-1, :],
-                                    in1=r2[:].rearrange("p h c -> p (h c)").unsqueeze(1).to_broadcast([P, 2, P // 2]), op=ALU.mult)
-            state["inv", b] = inv
+                                    in1=pairs_inv[:].unsqueeze(1).to_broadcast([P, 2, P // 2]), op=ALU.mult)
+            state["inv", b] = inv[:].rearrange("p h c -> p (h c)")
+
+        def miss_both(b):
+            tau = state["tau", b]
+            tau = tau[:].rearrange("p l w -> p w l")
+            g = goal_sb[b][:].rearrange("p (w l) -> p w l", l=2)
+            miss = work.tile([P, S // 2, 2], F32, name="miss")
+            both = work.tile([P, 2, S // 2], F32, name="both")
+            nc.vector.scalar_tensor_tensor(out=miss[:], in0=tau, scalar=-0.5, in1=g, op0=ALU.mult, op1=ALU.add)
+            nc.vector.scalar_tensor_tensor(out=both[:].rearrange("p l w -> p w l"), in0=tau, scalar=1.0, in1=g, op0=ALU.add, op1=ALU.mult)
+            squares = work.tile([P, D, RUNS], F32, name="squares")
+            nc.scalar.activation(out=squares[:].rearrange("p d v -> p v d"), in_=miss[:].rearrange("p (v h) l -> p v (h l)", h=2), func=ACT.Square, scale=0.5, bias=-0.25)
+            return both, [squares[:, d, :] for d in range(D)]
+
+        def denominator(b):
+            sum_tau = turned_sum("sum_tau", 1, stepped(state["tau", b]))
+            den = work.tile([P, P], F32, name="den")
+            nc.scalar.activation(out=den[:], in_=sum_tau[:], func=ACT.Copy, scale=-0.5, bias=-6.0)
+            state["den", b] = den
+
+        def elementwise(b):
+            both, squares = miss_both(b)
+            if b in L1_BLOCKS:
+                halves = work.tile([P, S // 2], F32, name="halves")
+                nc.vector.tensor_tensor(out=halves[:], in0=both[:, 0], in1=both[:, 1], op=ALU.add)
+                parts = [halves[:, 0::2], halves[:, 1::2]]
+            else:
+                parts = stepped(both)
+            state["both", b] = turned_sum("sum_both", 2, parts)
+            dd = turned_sum("dd", 2, squares)
+            dd_sb = work.tile([P, P], F32, name="dd_sb")
+            nc.scalar.copy(out=dd_sb[:], in_=dd[:])
+            state["dd", b] = dd_sb
 
         def finish(b):
             ratio = work.tile([P, P], F32, name="ratio")
             nc.vector.scalar_tensor_tensor(out=ratio[:], in0=state["both", b][:], scalar=1.0,
-                                           in1=state["inv", b][:].rearrange("p h c -> p (h c)"), op0=ALU.add, op1=ALU.mult)
-            loss = work.tile([P, P], F32, name="loss")
-            nc.vector.tensor_tensor(out=loss[:], in0=state["dd", b][:], in1=ratio[:], op=ALU.subtract)
-            turned = psum.tile([P, P], F32, name="turned", tag="turned", bufs=1)
-            nc.tensor.transpose(turned[:], loss[:], ident[:])
+                                           in1=state["inv", b], op0=ALU.add, op1=ALU.mult)
+            turned = turned_sum("turned", 1, [state["dd", b][:], ratio[:]])
             result = work.tile([P, P], F32, name="result")
             nc.scalar.copy(out=result[:], in_=turned[:])
             nc.sync.dma_start(out[b * P:(b + 1) * P, :], result[:])
 
+        def prepare(b):
+            grouped[b] = work.tile([P, PASSES, P, 4], BF16, name="grouped", bufs=1, align_bytes=64)
+            for o in range(PASSES):
+                cast(b, o, CAST_ENGINES[b][o])
+            quantize(b)
+
         nc.vector.tensor_copy(x_codes[0][:], table_words[0][:].indirect(offsets[:]))
         nc.vector.tensor_copy(x_planes[:], table_scales[:].indirect(offsets[:]))
-        cast(0, 0, "scalar")
-        cast(0, 1, "scalar")
-        quantize(0)
         nc.vector.tensor_copy(x_codes[1][:], table_words[1][:].indirect(offsets[:]))
+        grouped[0] = work.tile([P, PASSES, P, 4], BF16, name="grouped", bufs=1, align_bytes=64)
+        for o in range(PASSES):
+            cast(0, o, CAST_ENGINES[0][o])
+            quantize_pass(0, o)
         product(0)
+        prepare(1)
         for b in range(BLOCKS):
             if b + 1 < BLOCKS:
-                cast(b + 1, 0, "scalar")
-                cast(b + 1, 1, "scalar")
-                quantize(b + 1)
                 product(b + 1)
-            if b > 0:
-                finish(b - 1)
+            if b + 2 < BLOCKS:
+                prepare(b + 2)
+            denominator(b)
             elementwise(b)
             inverse(b)
-        finish(BLOCKS - 1)
+            finish(b)

@@ -17,39 +17,30 @@ ACT = mybir.ActivationFunctionType
 ALU = mybir.AluOpType
 
 P = 128
-PASSES = K // (4 * P)
-BLOCKS = V // P
+PACK = 4
+PASSES = K // (PACK * P)
+BANDS = V // P
 RUNS = S // D
-L1_BLOCKS = (0, 1)
-CAST_ENGINES = [["scalar","vector"],["scalar","vector"],["scalar","vector"],["scalar","vector"]]
+HALF = V // 2
 
 
 def tile_picked_ydice_dice_p_kernel(tc, x_words, x_scales, hT, goal, offs, out):
     nc = tc.nc
     with ExitStack() as ctx:
         keep = ctx.enter_context(tc.tile_pool(name="keep", bufs=1))
-        work = ctx.enter_context(tc.tile_pool(name="work", bufs=4))
         psum = ctx.enter_context(tc.psum_pool(name="psum", bufs=1))
 
         offsets = keep.tile([P, S // 16], U16, name="offsets")
-
         table_words = [keep.tile([P, T], U32, name="table_words%d" % o) for o in range(PASSES)]
         table_scales = keep.tile([P, T], U8, name="table_scales")
-        h_raw = [[keep.tile([P, 4, P], F32, name="h_raw%d_%d" % (b, o)) for o in range(PASSES)] for b in range(BLOCKS)]
-        goal_sb = [keep.tile([P, S], F32, name="goal%d" % b) for b in range(BLOCKS)]
+        h_first = keep.tile([P, PACK, V], F32, name="h_first")
+        h_second = [keep.tile([P, PACK, HALF], F32, name="h_second%d" % i) for i in range(2)]
+        goal_sb = [keep.tile([P, S], F32, name="goal%d" % b) for b in range(BANDS)]
         ident = keep.tile([P, P], F32, name="ident")
         nc.gpsimd.memset(table_scales[:].bitcast(I32), 0)
 
         def load_words(o):
             nc.sync.dma_start(table_words[o][:].bitcast(I32), x_words[o].rearrange("p c r -> p (c r)").bitcast(I32))
-
-        def load_h(b):
-            for o in range(PASSES):
-                rows = hT[o * 4 * P:(o + 1) * 4 * P, b * P:(b + 1) * P]
-                nc.sync.dma_start(h_raw[b][o][:], rows.rearrange("(p j) t -> p j t", j=4))
-
-        def load_goal(b):
-            nc.sync.dma_start(goal_sb[b][:], goal[b * P:(b + 1) * P, :])
 
         load_words(0)
         nc.sync.dma_start(offsets[:], offs)
@@ -57,132 +48,106 @@ def tile_picked_ydice_dice_p_kernel(tc, x_words, x_scales, hT, goal, offs, out):
             nc.sync.dma_start(table_scales[32 * q:32 * q + 4 * PASSES, :].bitcast(I32),
                               x_scales[:, 4 * q:4 * q + 4, :].bitcast(I32))
         make_identity(nc, ident[:])
+        nc.sync.dma_start(h_first[:], hT[0:PACK * P, :].rearrange("(p j) t -> p j t", j=PACK))
         load_words(1)
-        load_h(0)
-        for b in range(BLOCKS):
-            if b + 1 < BLOCKS:
-                load_h(b + 1)
-            load_goal(b)
+        for i in range(2):
+            rows = hT[PACK * P:2 * PACK * P, i * HALF:(i + 1) * HALF]
+            nc.sync.dma_start(h_second[i][:], rows.rearrange("(p j) t -> p j t", j=PACK))
+        for b in range(BANDS):
+            nc.sync.dma_start(goal_sb[b][:], goal[b * P:(b + 1) * P, :])
 
         x_codes = [keep.tile([P, S], U32, name="x_codes%d" % o, align_bytes=64) for o in range(PASSES)]
         x_planes = keep.tile([P, S], U8, name="x_planes", align_bytes=64)
-        h_codes = [keep.tile([P, PASSES * P], U32, name="h_codes%d" % b, align_bytes=64) for b in range(BLOCKS)]
-        h_planes = [keep.tile([P, PASSES * P], U8, name="h_planes%d" % b, align_bytes=64) for b in range(BLOCKS)]
-        grouped = {}
+        grouped = [[keep.tile([P, P, PACK], BF16, name="grouped%d_%d" % (o, b), align_bytes=64)
+                    for b in range(BANDS)] for o in range(PASSES)]
+        h_codes = [[keep.tile([P, P], U32, name="h_codes%d_%d" % (o, b), align_bytes=64)
+                    for b in range(BANDS)] for o in range(PASSES)]
+        h_planes = [[keep.tile([P, P], U8, name="h_planes%d_%d" % (o, b), align_bytes=64)
+                     for b in range(BANDS)] for o in range(PASSES)]
 
-        def cast(b, o, engine):
-            dst = grouped[b][:, o].rearrange("p (c i) j -> p c j i", i=4)
-            src = h_raw[b][o][:].rearrange("p j (c i) -> p c j i", i=4)
-            if engine == "vector":
-                nc.vector.tensor_copy(out=dst, in_=src)
-            else:
-                nc.scalar.copy(out=dst, in_=src)
+        def raw_band(o, b):
+            if o == 0:
+                return h_first[:, :, b * P:(b + 1) * P]
+            return h_second[b // 2][:, :, (b % 2) * P:(b % 2 + 1) * P]
 
-        def quantize(b):
-            nc.vector.quantize_mx(out=h_codes[b][:].bitcast(FP8X4), scales=h_planes[b][:],
-                                  in_=grouped[b][:].rearrange("p o t j -> p (o t j)"))
+        def interleave_on_scalar(o, b):
+            nc.scalar.copy(out=grouped[o][b][:], in_=raw_band(o, b).rearrange("p j t -> p t j"))
 
-        def quantize_pass(b, o):
-            cols = slice(o * P, (o + 1) * P)
-            nc.vector.quantize_mx(out=h_codes[b][:, cols].bitcast(FP8X4), scales=h_planes[b][:, cols],
-                                  in_=grouped[b][:, o].rearrange("p t j -> p (t j)"))
+        def interleave_on_vector(o, b):
+            nc.vector.tensor_copy(out=grouped[o][b][:].rearrange("p (c i) j -> p c j i", i=4),
+                                  in_=raw_band(o, b).rearrange("p j (c i) -> p c j i", i=4))
 
-        state = {}
+        def quantize(o, b):
+            nc.vector.quantize_mx(out=h_codes[o][b][:].bitcast(FP8X4), scales=h_planes[o][b][:],
+                                  in_=grouped[o][b][:].rearrange("p t j -> p (t j)"))
 
-        def product(b):
-            u = psum.tile([P, S], F32, name="u", tag="u", bufs=2)
-            for o in range(PASSES):
-                cols = slice(o * P, (o + 1) * P)
-                nc.tensor.matmul_mx(out=u[:], lhsT=h_codes[b][:, cols].bitcast(FP8X4), lhsT_scale=h_planes[b][:, cols],
-                                    rhs=x_codes[o][:].bitcast(FP8X4), rhs_scale=x_planes[4 * o:P, :],
-                                    start=(o == 0), stop=(o == PASSES - 1))
-            tau = work.tile([P, 2, S // 2], F32, name="tau")
-            nc.scalar.activation(out=tau[:], in_=u[:].rearrange("p (w l) -> p l w", l=2), func=ACT.Tanh, scale=0.5)
-            state["tau", b] = tau
+        scores = [psum.tile([P, S], F32, name="scores%d" % b, tag="band%d" % b) for b in range(BANDS)]
 
-        def turned_sum(tag, bufs, parts):
-            acc = psum.tile([P, P], F32, name=tag, tag=tag, bufs=bufs)
+        def product(o, b):
+            nc.tensor.matmul_mx(out=scores[b][:], lhsT=h_codes[o][b][:].bitcast(FP8X4), lhsT_scale=h_planes[o][b][:],
+                                rhs=x_codes[o][:].bitcast(FP8X4), rhs_scale=x_planes[4 * o:P, :],
+                                start=(o == 0), stop=(o == PASSES - 1))
+
+        def turned_sum(acc, parts):
             for n, part in enumerate(parts):
-                nc.tensor.matmul(out=acc[:], lhsT=part, rhs=ident[:], is_transpose=True,
+                nc.tensor.matmul(out=acc, lhsT=part, rhs=ident[:], is_transpose=True,
                                  start=(n == 0), stop=(n == len(parts) - 1))
-            return acc
 
-        def stepped(values):
-            return [values[:, l, h::2] for l in range(2) for h in range(2)]
-
-        def inverse(b):
-            den = state["den", b]
-            pairs = work.tile([P, P // 2], F32, name="pairs")
-            nc.vector.tensor_tensor(out=pairs[:], in0=den[:, 0:P // 2], in1=den[:, P // 2:P], op=ALU.mult)
-            pairs_inv = work.tile([P, P // 2], F32, name="pairs_inv")
-            nc.vector.reciprocal(out=pairs_inv[:], in_=pairs[:])
-            inv = work.tile([P, 2, P // 2], F32, name="inv")
-            nc.vector.tensor_tensor(out=inv[:], in0=den[:].rearrange("p (h c) -> p h c", h=2)[:, ::-1, :],
-                                    in1=pairs_inv[:].unsqueeze(1).to_broadcast([P, 2, P // 2]), op=ALU.mult)
-            state["inv", b] = inv[:].rearrange("p h c -> p (h c)")
-
-        def miss_both(b):
-            tau = state["tau", b]
-            tau = tau[:].rearrange("p l w -> p w l")
-            g = goal_sb[b][:].rearrange("p (w l) -> p w l", l=2)
-            miss = work.tile([P, S // 2, 2], F32, name="miss")
-            both = work.tile([P, 2, S // 2], F32, name="both")
-            nc.vector.scalar_tensor_tensor(out=miss[:], in0=tau, scalar=-0.5, in1=g, op0=ALU.mult, op1=ALU.add)
-            nc.vector.scalar_tensor_tensor(out=both[:].rearrange("p l w -> p w l"), in0=tau, scalar=1.0, in1=g, op0=ALU.add, op1=ALU.mult)
-            squares = work.tile([P, D, RUNS], F32, name="squares")
-            nc.scalar.activation(out=squares[:].rearrange("p d v -> p v d"), in_=miss[:].rearrange("p (v h) l -> p v (h l)", h=2), func=ACT.Square, scale=0.5, bias=-0.25)
-            return both, [squares[:, d, :] for d in range(D)]
-
-        def denominator(b):
-            sum_tau = turned_sum("sum_tau", 1, stepped(state["tau", b]))
-            den = work.tile([P, P], F32, name="den")
-            nc.scalar.activation(out=den[:], in_=sum_tau[:], func=ACT.Copy, scale=-0.5, bias=-6.0)
-            state["den", b] = den
-
-        def elementwise(b):
-            both, squares = miss_both(b)
-            if b in L1_BLOCKS:
-                halves = work.tile([P, S // 2], F32, name="halves")
-                nc.vector.tensor_tensor(out=halves[:], in0=both[:, 0], in1=both[:, 1], op=ALU.add)
-                parts = [halves[:, 0::2], halves[:, 1::2]]
-            else:
-                parts = stepped(both)
-            state["both", b] = turned_sum("sum_both", 2, parts)
-            dd = turned_sum("dd", 2, squares)
-            dd_sb = work.tile([P, P], F32, name="dd_sb")
-            nc.scalar.copy(out=dd_sb[:], in_=dd[:])
-            state["dd", b] = dd_sb
-
-        def finish(b):
-            ratio = work.tile([P, P], F32, name="ratio")
-            nc.vector.scalar_tensor_tensor(out=ratio[:], in0=state["both", b][:], scalar=1.0,
-                                           in1=state["inv", b], op0=ALU.add, op1=ALU.mult)
-            turned = turned_sum("turned", 1, [state["dd", b][:], ratio[:]])
-            result = work.tile([P, P], F32, name="result")
-            nc.scalar.copy(out=result[:], in_=turned[:])
-            nc.sync.dma_start(out[b * P:(b + 1) * P, :], result[:])
-
-        def prepare(b):
-            grouped[b] = work.tile([P, PASSES, P, 4], BF16, name="grouped", bufs=1, align_bytes=64)
-            for o in range(PASSES):
-                cast(b, o, CAST_ENGINES[b][o])
-            quantize(b)
+        def planes_of(tile):
+            return [tile[:, d, :] for d in range(D)]
 
         nc.vector.tensor_copy(x_codes[0][:], table_words[0][:].indirect(offsets[:]))
         nc.vector.tensor_copy(x_planes[:], table_scales[:].indirect(offsets[:]))
+
+        def prepare_pair(o, pair):
+            interleave_on_vector(o, 2 * pair)
+            interleave_on_scalar(o, 2 * pair + 1)
+            for b in (2 * pair, 2 * pair + 1):
+                quantize(o, b)
+                product(o, b)
+
+        for pair in range(2):
+            prepare_pair(0, pair)
         nc.vector.tensor_copy(x_codes[1][:], table_words[1][:].indirect(offsets[:]))
-        grouped[0] = work.tile([P, PASSES, P, 4], BF16, name="grouped", bufs=1, align_bytes=64)
-        for o in range(PASSES):
-            cast(0, o, CAST_ENGINES[0][o])
-            quantize_pass(0, o)
-        product(0)
-        prepare(1)
-        for b in range(BLOCKS):
-            if b + 1 < BLOCKS:
-                product(b + 1)
-            if b + 2 < BLOCKS:
-                prepare(b + 2)
-            denominator(b)
-            elementwise(b)
-            inverse(b)
-            finish(b)
+        for pair in range(2):
+            prepare_pair(1, pair)
+
+        prob = [keep.tile([P, D, RUNS], F32, name="prob%d" % b) for b in range(BANDS)]
+        both = [keep.tile([P, D, RUNS], F32, name="both%d" % b) for b in range(BANDS)]
+        miss = [keep.tile([P, RUNS, D], F32, name="miss%d" % b) for b in range(BANDS)]
+        squares = [keep.tile([P, D, RUNS], F32, name="squares%d" % b) for b in range(BANDS)]
+        sum_prob = psum.tile([P, V], F32, name="sum_prob")
+        sum_both = psum.tile([P, V], F32, name="sum_both")
+        for b in range(BANDS):
+            nc.scalar.activation(out=prob[b][:], in_=scores[b][:].rearrange("p (v d) -> p d v", d=D), func=ACT.Tanh,
+                                 scale=0.5)
+            turned_sum(sum_prob[:, b * P:(b + 1) * P], planes_of(prob[b]))
+        for b in range(BANDS):
+            g = goal_sb[b][:].rearrange("p (v d) -> p v d", d=D)
+            p_by_run = prob[b][:].rearrange("p d v -> p v d")
+            nc.vector.scalar_tensor_tensor(out=both[b][:].rearrange("p d v -> p v d"), in0=p_by_run, scalar=1.0, in1=g,
+                                           op0=ALU.add, op1=ALU.mult)
+            turned_sum(sum_both[:, b * P:(b + 1) * P], planes_of(both[b]))
+            nc.vector.scalar_tensor_tensor(out=miss[b][:], in0=p_by_run, scalar=-0.5, in1=g, op0=ALU.mult, op1=ALU.add)
+
+        root = keep.tile([P, V], F32, name="root")
+        nc.scalar.activation(out=root[:], in_=sum_prob[:], func=ACT.Abs_reciprocal_sqrt, scale=0.5, bias=6.0)
+        half_ratio = keep.tile([P, V], F32, name="half_ratio")
+        nc.vector.scalar_tensor_tensor(out=half_ratio[:], in0=sum_both[:], scalar=1.0, in1=root[:],
+                                       op0=ALU.add, op1=ALU.mult)
+        ratio = keep.tile([P, V], F32, name="ratio")
+        nc.vector.tensor_tensor(out=ratio[:], in0=half_ratio[:], in1=root[:], op=ALU.mult)
+        for b in range(BANDS):
+            cols = slice(b * P, (b + 1) * P)
+            nc.scalar.activation(out=squares[b][:].rearrange("p d v -> p v d"),
+                                 in_=miss[b][:], func=ACT.Square, bias=-0.5)
+            sum_squares = psum.tile([P, P], F32, name="sum_squares%d" % b, tag="band%d" % b)
+            turned_sum(sum_squares[:], planes_of(squares[b]))
+            loss = keep.tile([P, P], F32, name="loss%d" % b)
+            nc.vector.scalar_tensor_tensor(out=loss[:], in0=sum_squares[:], scalar=1.0 / D, in1=ratio[:, cols],
+                                           op0=ALU.mult, op1=ALU.subtract)
+            turned = psum.tile([P, P], F32, name="turned", tag="turned", bufs=2)
+            nc.tensor.transpose(turned[:], loss[:], ident[:])
+            result = keep.tile([P, P], F32, name="result%d" % b)
+            nc.scalar.copy(out=result[:], in_=turned[:])
+            nc.sync.dma_start(out[b * P:(b + 1) * P, :], result[:])

@@ -22,19 +22,23 @@ PASSES = K // (PACK * P)
 BANDS = V // P
 RUNS = S // D
 HALF = V // 2
+BAND_BYTES = S * 4
 
 
 def tile_picked_ydice_dice_p_kernel(tc, x_words, x_scales, hT, goal, offs, out):
     nc = tc.nc
     with ExitStack() as ctx:
         keep = ctx.enter_context(tc.tile_pool(name="keep", bufs=1))
+        late = ctx.enter_context(tc.tile_pool(name="late", bufs=1))
+        reuse = ctx.enter_context(tc.tile_pool(name="reuse", bufs=1))
         psum = ctx.enter_context(tc.psum_pool(name="psum", bufs=1))
 
         offsets = keep.tile([P, S // 16], U16, name="offsets")
         table_words = [keep.tile([P, T], U32, name="table_words%d" % o) for o in range(PASSES)]
         table_scales = keep.tile([P, T], U8, name="table_scales")
         h_first = keep.tile([P, PACK, V], F32, name="h_first")
-        h_second = [keep.tile([P, PACK, HALF], F32, name="h_second%d" % i) for i in range(2)]
+        h_second = [keep.tile([P, PACK, HALF], F32, name="h_second0"),
+                    reuse.tile([P, PACK, HALF], F32, name="h_second1", offset=0)]
         goal_sb = [keep.tile([P, S], F32, name="goal%d" % b) for b in range(BANDS)]
         ident = keep.tile([P, P], F32, name="ident")
         nc.gpsimd.memset(table_scales[:].bitcast(I32), 0)
@@ -60,6 +64,7 @@ def tile_picked_ydice_dice_p_kernel(tc, x_words, x_scales, hT, goal, offs, out):
         x_planes = keep.tile([P, S], U8, name="x_planes", align_bytes=64)
         grouped = [[keep.tile([P, P, PACK], BF16, name="grouped%d_%d" % (o, b), align_bytes=64)
                     for b in range(BANDS)] for o in range(PASSES)]
+        grouped[1][3] = reuse.tile([P, P, PACK], BF16, name="grouped_last", align_bytes=64, offset=3 * BAND_BYTES - 512)
         h_codes = [[keep.tile([P, P], U32, name="h_codes%d_%d" % (o, b), align_bytes=64)
                     for b in range(BANDS)] for o in range(PASSES)]
         h_planes = [[keep.tile([P, P], U8, name="h_planes%d_%d" % (o, b), align_bytes=64)
@@ -115,8 +120,11 @@ def tile_picked_ydice_dice_p_kernel(tc, x_words, x_scales, hT, goal, offs, out):
         prob = [keep.tile([P, D, RUNS], F32, name="prob%d" % b) for b in range(BANDS)]
         both = [keep.tile([P, D, RUNS], F32, name="both%d" % b) for b in range(BANDS)]
         miss = [keep.tile([P, RUNS, D], F32, name="miss%d" % b) for b in range(BANDS)]
-        squares = [keep.tile([P, D, RUNS], F32, name="squares%d" % b) for b in range(BANDS)]
-        sum_prob = psum.tile([P, V], F32, name="sum_prob")
+        for b in range(2):
+            prob[b] = reuse.tile([P, D, RUNS], F32, name="prob_early%d" % b, offset=b * BAND_BYTES)
+        both[0] = reuse.tile([P, D, RUNS], F32, name="both_first", offset=2 * BAND_BYTES)
+        miss[0] = reuse.tile([P, RUNS, D], F32, name="miss_first", offset=3 * BAND_BYTES)
+        sum_prob = psum.tile([P, V], F32, name="sum_prob", tag="sum_prob")
         sum_both = psum.tile([P, V], F32, name="sum_both")
         for b in range(BANDS):
             nc.scalar.activation(out=prob[b][:], in_=scores[b][:].rearrange("p (v d) -> p d v", d=D), func=ACT.Tanh,
@@ -131,23 +139,62 @@ def tile_picked_ydice_dice_p_kernel(tc, x_words, x_scales, hT, goal, offs, out):
             nc.vector.scalar_tensor_tensor(out=miss[b][:], in0=p_by_run, scalar=-0.5, in1=g, op0=ALU.mult, op1=ALU.add)
 
         root = keep.tile([P, V], F32, name="root")
-        nc.scalar.activation(out=root[:], in_=sum_prob[:], func=ACT.Abs_reciprocal_sqrt, scale=0.5, bias=6.0)
+        six = late.tile([P, (BANDS - 1) * S], F32, name="six", offset=0)
+        nc.gpsimd.memset(six[:, 0:1], 6.0)
+        nc.scalar.activation(out=root[:], in_=sum_prob[:], func=ACT.Abs_reciprocal_sqrt, scale=0.5, bias=six[:, 0:1])
+        squares = [late.tile([P, S], F32, name="squares%d" % b, offset=(b - 1) * BAND_BYTES) for b in range(1, BANDS)]
+        squares.insert(0, keep.tile([P, S], F32, name="squares_first"))
+        vector_share = keep.tile([P, 2, RUNS], F32, name="vector_share")
+        def square_planes(b):
+            return squares[b][:].rearrange("p (d v) -> p d v", d=D)
+
+        last = BANDS - 1
+        nc.vector.scalar_tensor_tensor(out=vector_share[:].rearrange("p d v -> p v d"), in0=miss[last][:, :, 0:2], scalar=-1.0,
+                                       in1=miss[last][:, :, 0:2], op0=ALU.add, op1=ALU.mult)
+        sum_squares = {last: psum.tile([P, P], F32, name="sum_squares_last", tag="band%d" % last)}
+
         half_ratio = keep.tile([P, V], F32, name="half_ratio")
-        nc.vector.scalar_tensor_tensor(out=half_ratio[:], in0=sum_both[:], scalar=1.0, in1=root[:],
-                                       op0=ALU.add, op1=ALU.mult)
         ratio = keep.tile([P, V], F32, name="ratio")
-        nc.vector.tensor_tensor(out=ratio[:], in0=half_ratio[:], in1=root[:], op=ALU.mult)
-        for b in range(BANDS):
+        for pair in range(2):
+            cols = slice(pair * HALF, (pair + 1) * HALF)
+            nc.vector.scalar_tensor_tensor(out=half_ratio[:, cols], in0=sum_both[:, cols], scalar=1.0, in1=root[:, cols],
+                                           op0=ALU.add, op1=ALU.mult)
+        for pair in range(2):
+            cols = slice(pair * HALF, (pair + 1) * HALF)
+            nc.vector.scalar_tensor_tensor(out=ratio[:, cols], in0=half_ratio[:, cols], scalar=-1.0, in1=root[:, cols],
+                                           op0=ALU.mult, op1=ALU.mult)
+
+        first_pair = psum.tile([P, HALF], F32, name="first_pair", tag="band0")
+        sum_squares[2] = psum.tile([P, P], F32, name="sum_squares2", tag="band2")
+        targets = [first_pair[:, 0:P], first_pair[:, P:HALF], sum_squares[2][:]]
+        for b in range(last):
+            nc.scalar.activation(out=square_planes(b).rearrange("p d v -> p v d"), in_=miss[b][:], func=ACT.Square, bias=-0.5)
+            turned_sum(targets[b], planes_of(square_planes(b)))
+        nc.scalar.activation(out=square_planes(last)[:, 2:4, :].rearrange("p d v -> p v d"), in_=miss[last][:, :, 2:4],
+                             func=ACT.Square, bias=-0.5)
+        turned_sum(sum_squares[last][:], [vector_share[:, 0, :], vector_share[:, 1, :],
+                                          square_planes(last)[:, 2, :], square_planes(last)[:, 3, :]])
+
+        error = keep.tile([P, HALF], F32, name="error")
+        nc.scalar.activation(out=error[:], in_=first_pair[:], func=ACT.Copy, scale=1.0 / D)
+        turned_pair = psum.tile([P, HALF], F32, name="turned_pair", tag="turned0")
+        for b in range(2):
             cols = slice(b * P, (b + 1) * P)
-            nc.scalar.activation(out=squares[b][:].rearrange("p d v -> p v d"),
-                                 in_=miss[b][:], func=ACT.Square, bias=-0.5)
-            sum_squares = psum.tile([P, P], F32, name="sum_squares%d" % b, tag="band%d" % b)
-            turned_sum(sum_squares[:], planes_of(squares[b]))
+            turned_sum(turned_pair[:, cols], [error[:, cols], ratio[:, cols]])
+        result_pair = keep.tile([P, 2, P], F32, name="result_pair")
+        nc.scalar.copy(out=result_pair[:].rearrange("p n v -> p (n v)"), in_=turned_pair[:])
+        nc.scalar.dma_start(out[0:HALF, :].rearrange("(n p) v -> p n v", p=P), result_pair[:])
+
+        for b in (2, last):
+            cols = slice(b * P, (b + 1) * P)
             loss = keep.tile([P, P], F32, name="loss%d" % b)
-            nc.vector.scalar_tensor_tensor(out=loss[:], in0=sum_squares[:], scalar=1.0 / D, in1=ratio[:, cols],
-                                           op0=ALU.mult, op1=ALU.subtract)
-            turned = psum.tile([P, P], F32, name="turned", tag="turned", bufs=2)
+            nc.vector.scalar_tensor_tensor(out=loss[:], in0=sum_squares[b][:], scalar=1.0 / D, in1=ratio[:, cols],
+                                           op0=ALU.mult, op1=ALU.add)
+            turned = psum.tile([P, P], F32, name="turned%d" % b, tag=("band1" if b == last else "turned1"))
             nc.tensor.transpose(turned[:], loss[:], ident[:])
             result = keep.tile([P, P], F32, name="result%d" % b)
-            nc.scalar.copy(out=result[:], in_=turned[:])
-            nc.sync.dma_start(out[b * P:(b + 1) * P, :], result[:])
+            if b == last:
+                nc.scalar.activation(out=result[:], in_=turned[:], func=ACT.Copy, bias=0.5 / D)
+            else:
+                nc.vector.tensor_copy(out=result[:], in_=turned[:])
+            (nc.scalar if b == last else nc.sync).dma_start(out[cols, :], result[:])

@@ -183,7 +183,7 @@ def tile_picked_ydice_dice_p_kernel(tc, x_words, x_scales, hT, goal, offs, out):
             turned_sum(turned_pair[:, cols], [error[:, cols], ratio[:, cols]])
         result_pair = keep.tile([P, 2, P], F32, name="result_pair")
         nc.scalar.copy(out=result_pair[:].rearrange("p n v -> p (n v)"), in_=turned_pair[:])
-        nc.scalar.dma_start(out[0:HALF, :].rearrange("(n p) v -> p n v", p=P), result_pair[:])
+        nc.sync.dma_start(out[0:HALF, :].rearrange("(n p) v -> p n v", p=P), result_pair[:])
 
         for b in (2, last):
             cols = slice(b * P, (b + 1) * P)
@@ -197,4 +197,4 @@ def tile_picked_ydice_dice_p_kernel(tc, x_words, x_scales, hT, goal, offs, out):
                 nc.scalar.activation(out=result[:], in_=turned[:], func=ACT.Copy, bias=0.5 / D)
             else:
                 nc.vector.tensor_copy(out=result[:], in_=turned[:])
-            (nc.scalar if b == last else nc.sync).dma_start(out[cols, :], result[:])
+            nc.sync.dma_start(out[cols, :], result[:])

@@ -117,26 +117,26 @@ def tile_picked_ydice_dice_p_kernel(tc, x_words, x_scales, hT, goal, offs, out):
         for pair in range(2):
             prepare_pair(1, pair)
 
-        prob = [keep.tile([P, D, RUNS], F32, name="prob%d" % b) for b in range(BANDS)]
+        prob = [keep.tile([P, 2, S // 2], F32, name="prob%d" % b) for b in range(BANDS)]
         both = [keep.tile([P, D, RUNS], F32, name="both%d" % b) for b in range(BANDS)]
         miss = [keep.tile([P, RUNS, D], F32, name="miss%d" % b) for b in range(BANDS)]
         for b in range(2):
-            prob[b] = reuse.tile([P, D, RUNS], F32, name="prob_early%d" % b, offset=b * BAND_BYTES)
+            prob[b] = reuse.tile([P, 2, S // 2], F32, name="prob_early%d" % b, offset=b * BAND_BYTES)
         both[0] = reuse.tile([P, D, RUNS], F32, name="both_first", offset=2 * BAND_BYTES)
         miss[0] = reuse.tile([P, RUNS, D], F32, name="miss_first", offset=3 * BAND_BYTES)
         sum_prob = psum.tile([P, V], F32, name="sum_prob", tag="sum_prob")
         sum_both = psum.tile([P, V], F32, name="sum_both")
         for b in range(BANDS):
-            nc.scalar.activation(out=prob[b][:], in_=scores[b][:].rearrange("p (v d) -> p d v", d=D), func=ACT.Tanh,
+            nc.scalar.activation(out=prob[b][:], in_=scores[b][:].rearrange("p (w l) -> p l w", l=2), func=ACT.Tanh,
                                  scale=0.5)
-            turned_sum(sum_prob[:, b * P:(b + 1) * P], planes_of(prob[b]))
+            turned_sum(sum_prob[:, b * P:(b + 1) * P], [prob[b][:, l, h::2] for l in range(2) for h in range(2)])
         for b in range(BANDS):
-            g = goal_sb[b][:].rearrange("p (v d) -> p v d", d=D)
-            p_by_run = prob[b][:].rearrange("p d v -> p v d")
+            g = goal_sb[b][:].rearrange("p (w l) -> p w l", l=2)
+            p_by_run = prob[b][:].rearrange("p l w -> p w l")
             nc.vector.scalar_tensor_tensor(out=both[b][:].rearrange("p d v -> p v d"), in0=p_by_run, scalar=1.0, in1=g,
                                            op0=ALU.add, op1=ALU.mult)
             turned_sum(sum_both[:, b * P:(b + 1) * P], planes_of(both[b]))
-            nc.vector.scalar_tensor_tensor(out=miss[b][:], in0=p_by_run, scalar=-0.5, in1=g, op0=ALU.mult, op1=ALU.add)
+            nc.vector.scalar_tensor_tensor(out=miss[b][:].rearrange("p v (h l) -> p (v h) l", l=2), in0=p_by_run, scalar=-0.5, in1=g, op0=ALU.mult, op1=ALU.add)
 
         root = keep.tile([P, V], F32, name="root")
         six = late.tile([P, (BANDS - 1) * S], F32, name="six", offset=0)

@@ -20,9 +20,12 @@ P = 128
 PACK = 4
 PASSES = K // (PACK * P)
 BANDS = V // P
+LAST = BANDS - 1
 RUNS = S // D
 HALF = V // 2
 BAND_BYTES = S * 4
+GROUPED_BYTES = P * PACK * 2
+SHARE = D // 2
 
 
 def tile_picked_ydice_dice_p_kernel(tc, x_words, x_scales, hT, goal, offs, out):
@@ -54,147 +57,158 @@ def tile_picked_ydice_dice_p_kernel(tc, x_words, x_scales, hT, goal, offs, out):
         make_identity(nc, ident[:])
         nc.sync.dma_start(h_first[:], hT[0:PACK * P, :].rearrange("(p j) t -> p j t", j=PACK))
         load_words(1)
-        for i in range(2):
-            rows = hT[PACK * P:2 * PACK * P, i * HALF:(i + 1) * HALF]
-            nc.sync.dma_start(h_second[i][:], rows.rearrange("(p j) t -> p j t", j=PACK))
+        for pair in range(2):
+            rows = hT[PACK * P:2 * PACK * P, pair * HALF:(pair + 1) * HALF]
+            nc.sync.dma_start(h_second[pair][:], rows.rearrange("(p j) t -> p j t", j=PACK))
         for b in range(BANDS):
             nc.sync.dma_start(goal_sb[b][:], goal[b * P:(b + 1) * P, :])
 
         x_codes = [keep.tile([P, S], U32, name="x_codes%d" % o, align_bytes=64) for o in range(PASSES)]
-        x_planes = keep.tile([P, S], U8, name="x_planes", align_bytes=64)
-        grouped = [[keep.tile([P, P, PACK], BF16, name="grouped%d_%d" % (o, b), align_bytes=64)
-                    for b in range(BANDS)] for o in range(PASSES)]
-        grouped[1][3] = reuse.tile([P, P, PACK], BF16, name="grouped_last", align_bytes=64, offset=3 * BAND_BYTES - 512)
+        x_scale_rows = keep.tile([P, S], U8, name="x_scale_rows", align_bytes=64)
+
+        def grouped_tile(o, b):
+            name = "grouped%d_%d" % (o, b)
+            if (o, b) == (PASSES - 1, LAST):
+                return reuse.tile([P, P, PACK], BF16, name=name, align_bytes=64,
+                                  offset=3 * BAND_BYTES - GROUPED_BYTES // 2)
+            return keep.tile([P, P, PACK], BF16, name=name, align_bytes=64)
+
+        grouped = [[grouped_tile(o, b) for b in range(BANDS)] for o in range(PASSES)]
         h_codes = [[keep.tile([P, P], U32, name="h_codes%d_%d" % (o, b), align_bytes=64)
                     for b in range(BANDS)] for o in range(PASSES)]
-        h_planes = [[keep.tile([P, P], U8, name="h_planes%d_%d" % (o, b), align_bytes=64)
-                     for b in range(BANDS)] for o in range(PASSES)]
+        h_scale_rows = [[keep.tile([P, P], U8, name="h_scale_rows%d_%d" % (o, b), align_bytes=64)
+                         for b in range(BANDS)] for o in range(PASSES)]
+        scores = [psum.tile([P, S], F32, name="scores%d" % b, tag="band%d" % b) for b in range(BANDS)]
 
         def raw_band(o, b):
             if o == 0:
                 return h_first[:, :, b * P:(b + 1) * P]
             return h_second[b // 2][:, :, (b % 2) * P:(b % 2 + 1) * P]
 
-        def interleave_on_scalar(o, b):
-            nc.scalar.copy(out=grouped[o][b][:], in_=raw_band(o, b).rearrange("p j t -> p t j"))
-
-        def interleave_on_vector(o, b):
-            nc.vector.tensor_copy(out=grouped[o][b][:].rearrange("p (c i) j -> p c j i", i=4),
-                                  in_=raw_band(o, b).rearrange("p j (c i) -> p c j i", i=4))
-
-        def quantize(o, b):
-            nc.vector.quantize_mx(out=h_codes[o][b][:].bitcast(FP8X4), scales=h_planes[o][b][:],
-                                  in_=grouped[o][b][:].rearrange("p t j -> p (t j)"))
-
-        scores = [psum.tile([P, S], F32, name="scores%d" % b, tag="band%d" % b) for b in range(BANDS)]
-
-        def product(o, b):
-            nc.tensor.matmul_mx(out=scores[b][:], lhsT=h_codes[o][b][:].bitcast(FP8X4), lhsT_scale=h_planes[o][b][:],
-                                rhs=x_codes[o][:].bitcast(FP8X4), rhs_scale=x_planes[4 * o:P, :],
-                                start=(o == 0), stop=(o == PASSES - 1))
-
-        def turned_sum(acc, parts):
-            for n, part in enumerate(parts):
-                nc.tensor.matmul(out=acc, lhsT=part, rhs=ident[:], is_transpose=True,
-                                 start=(n == 0), stop=(n == len(parts) - 1))
-
-        def planes_of(tile):
-            return [tile[:, d, :] for d in range(D)]
+        def prepare_pair(o, pair):
+            even, odd = 2 * pair, 2 * pair + 1
+            nc.vector.tensor_copy(out=grouped[o][even][:].rearrange("p (c i) j -> p c j i", i=4),
+                                  in_=raw_band(o, even).rearrange("p j (c i) -> p c j i", i=4))
+            nc.scalar.copy(out=grouped[o][odd][:], in_=raw_band(o, odd).rearrange("p j t -> p t j"))
+            for b in (even, odd):
+                nc.vector.quantize_mx(out=h_codes[o][b][:].bitcast(FP8X4), scales=h_scale_rows[o][b][:],
+                                      in_=grouped[o][b][:].rearrange("p t j -> p (t j)"))
+                nc.tensor.matmul_mx(out=scores[b][:], lhsT=h_codes[o][b][:].bitcast(FP8X4),
+                                    lhsT_scale=h_scale_rows[o][b][:], rhs=x_codes[o][:].bitcast(FP8X4),
+                                    rhs_scale=x_scale_rows[4 * o:P, :], start=(o == 0), stop=(o == PASSES - 1))
 
         nc.vector.tensor_copy(x_codes[0][:], table_words[0][:].indirect(offsets[:]))
-        nc.vector.tensor_copy(x_planes[:], table_scales[:].indirect(offsets[:]))
-
-        def prepare_pair(o, pair):
-            interleave_on_vector(o, 2 * pair)
-            interleave_on_scalar(o, 2 * pair + 1)
-            for b in (2 * pair, 2 * pair + 1):
-                quantize(o, b)
-                product(o, b)
-
+        nc.vector.tensor_copy(x_scale_rows[:], table_scales[:].indirect(offsets[:]))
         for pair in range(2):
             prepare_pair(0, pair)
         nc.vector.tensor_copy(x_codes[1][:], table_words[1][:].indirect(offsets[:]))
         for pair in range(2):
             prepare_pair(1, pair)
 
-        prob = [keep.tile([P, 2, S // 2], F32, name="prob%d" % b) for b in range(BANDS)]
-        both = [keep.tile([P, D, RUNS], F32, name="both%d" % b) for b in range(BANDS)]
-        miss = [keep.tile([P, RUNS, D], F32, name="miss%d" % b) for b in range(BANDS)]
-        for b in range(2):
-            prob[b] = reuse.tile([P, 2, S // 2], F32, name="prob_early%d" % b, offset=b * BAND_BYTES)
-        both[0] = reuse.tile([P, D, RUNS], F32, name="both_first", offset=2 * BAND_BYTES)
-        miss[0] = reuse.tile([P, RUNS, D], F32, name="miss_first", offset=3 * BAND_BYTES)
-        sum_prob = psum.tile([P, V], F32, name="sum_prob", tag="sum_prob")
-        sum_both = psum.tile([P, V], F32, name="sum_both")
+        def turned_sum(acc, parts):
+            for n, part in enumerate(parts):
+                nc.tensor.matmul(out=acc, lhsT=part, rhs=ident[:], is_transpose=True,
+                                 start=(n == 0), stop=(n == len(parts) - 1))
+
+        def band_tile(name, b, shape, reused):
+            if b in reused:
+                return reuse.tile(shape, F32, name="%s%d" % (name, b), offset=reused[b] * BAND_BYTES)
+            return keep.tile(shape, F32, name="%s%d" % (name, b))
+
+        tau = [band_tile("tau", b, [P, 2, S // 2], {0: 0, 1: 1}) for b in range(BANDS)]
+        overlap = [band_tile("overlap", b, [P, D, RUNS], {0: 2}) for b in range(BANDS)]
+        shifted = [band_tile("shifted", b, [P, RUNS, D], {0: 3}) for b in range(BANDS)]
+        sum_tau = psum.tile([P, V], F32, name="sum_tau", tag="sum_tau")
+        sum_overlap = [psum.tile([P, HALF], F32, name="sum_overlap%d" % pair, tag="sum_overlap%d" % pair)
+                       for pair in range(2)]
         for b in range(BANDS):
-            nc.scalar.activation(out=prob[b][:], in_=scores[b][:].rearrange("p (w l) -> p l w", l=2), func=ACT.Tanh,
+            nc.scalar.activation(out=tau[b][:], in_=scores[b][:].rearrange("p (w l) -> p l w", l=2), func=ACT.Tanh,
                                  scale=0.5)
-            turned_sum(sum_prob[:, b * P:(b + 1) * P], [prob[b][:, l, h::2] for l in range(2) for h in range(2)])
-        for b in range(BANDS):
-            g = goal_sb[b][:].rearrange("p (w l) -> p w l", l=2)
-            p_by_run = prob[b][:].rearrange("p l w -> p w l")
-            nc.vector.scalar_tensor_tensor(out=both[b][:].rearrange("p d v -> p v d"), in0=p_by_run, scalar=1.0, in1=g,
-                                           op0=ALU.add, op1=ALU.mult)
-            turned_sum(sum_both[:, b * P:(b + 1) * P], planes_of(both[b]))
-            nc.vector.scalar_tensor_tensor(out=miss[b][:].rearrange("p v (h l) -> p (v h) l", l=2), in0=p_by_run, scalar=-0.5, in1=g, op0=ALU.mult, op1=ALU.add)
+            turned_sum(sum_tau[:, b * P:(b + 1) * P], [tau[b][:, l, h::2] for l in range(2) for h in range(2)])
+
+        def in_point_order(b):
+            return tau[b][:].rearrange("p l w -> p w l"), goal_sb[b][:].rearrange("p (w l) -> p w l", l=2)
+
+        def make_overlap(b):
+            tau_points, goal_points = in_point_order(b)
+            nc.vector.scalar_tensor_tensor(out=overlap[b][:].rearrange("p d v -> p v d"), in0=tau_points, scalar=1.0,
+                                           in1=goal_points, op0=ALU.add, op1=ALU.mult)
+            turned_sum(sum_overlap[b // 2][:, (b % 2) * P:(b % 2 + 1) * P], [overlap[b][:, d, :] for d in range(D)])
+
+        def make_shifted(b):
+            tau_points, goal_points = in_point_order(b)
+            nc.vector.scalar_tensor_tensor(out=shifted[b][:].rearrange("p v (h l) -> p (v h) l", l=2), in0=tau_points,
+                                           scalar=-0.5, in1=goal_points, op0=ALU.mult, op1=ALU.add)
+
+        make_overlap(0)
+        make_shifted(0)
+        for b in range(1, BANDS):
+            make_overlap(b)
+        for b in range(1, BANDS):
+            make_shifted(b)
 
         root = keep.tile([P, V], F32, name="root")
-        six = late.tile([P, (BANDS - 1) * S], F32, name="six", offset=0)
+        six = late.tile([P, LAST * S], F32, name="six", offset=0)
         nc.gpsimd.memset(six[:, 0:1], 6.0)
-        nc.scalar.activation(out=root[:], in_=sum_prob[:], func=ACT.Abs_reciprocal_sqrt, scale=0.5, bias=six[:, 0:1])
-        squares = [late.tile([P, S], F32, name="squares%d" % b, offset=(b - 1) * BAND_BYTES) for b in range(1, BANDS)]
-        squares.insert(0, keep.tile([P, S], F32, name="squares_first"))
-        vector_share = keep.tile([P, 2, RUNS], F32, name="vector_share")
-        def square_planes(b):
-            return squares[b][:].rearrange("p (d v) -> p d v", d=D)
-
-        last = BANDS - 1
-        nc.vector.scalar_tensor_tensor(out=vector_share[:].rearrange("p d v -> p v d"), in0=miss[last][:, :, 0:2], scalar=-1.0,
-                                       in1=miss[last][:, :, 0:2], op0=ALU.add, op1=ALU.mult)
-        sum_squares = {last: psum.tile([P, P], F32, name="sum_squares_last", tag="band%d" % last)}
-
+        nc.scalar.activation(out=root[:], in_=sum_tau[:], func=ACT.Abs_reciprocal_sqrt, scale=0.5, bias=six[:, 0:1])
+        squares = [keep.tile([P, D, RUNS], F32, name="squares0")]
+        squares.extend(late.tile([P, D, RUNS], F32, name="squares%d" % b, offset=(b - 1) * BAND_BYTES)
+                       for b in range(1, BANDS))
+        vector_squares = keep.tile([P, SHARE, RUNS], F32, name="vector_squares")
+        sum_last = psum.tile([P, P], F32, name="sum_last", tag="band%d" % LAST)
         half_ratio = keep.tile([P, V], F32, name="half_ratio")
-        ratio = keep.tile([P, V], F32, name="ratio")
-        for pair in range(2):
+        minus_ratio = keep.tile([P, V], F32, name="minus_ratio")
+
+        def make_half_ratio(pair):
             cols = slice(pair * HALF, (pair + 1) * HALF)
-            nc.vector.scalar_tensor_tensor(out=half_ratio[:, cols], in0=sum_both[:, cols], scalar=1.0, in1=root[:, cols],
-                                           op0=ALU.add, op1=ALU.mult)
-        for pair in range(2):
+            nc.vector.scalar_tensor_tensor(out=half_ratio[:, cols], in0=sum_overlap[pair][:], scalar=1.0,
+                                           in1=root[:, cols], op0=ALU.add, op1=ALU.mult)
+
+        def make_minus_ratio(pair):
             cols = slice(pair * HALF, (pair + 1) * HALF)
-            nc.vector.scalar_tensor_tensor(out=ratio[:, cols], in0=half_ratio[:, cols], scalar=-1.0, in1=root[:, cols],
-                                           op0=ALU.mult, op1=ALU.mult)
+            nc.vector.scalar_tensor_tensor(out=minus_ratio[:, cols], in0=half_ratio[:, cols], scalar=-1.0,
+                                           in1=root[:, cols], op0=ALU.mult, op1=ALU.mult)
 
-        first_pair = psum.tile([P, HALF], F32, name="first_pair", tag="band0")
-        sum_squares[2] = psum.tile([P, P], F32, name="sum_squares2", tag="band2")
-        targets = [first_pair[:, 0:P], first_pair[:, P:HALF], sum_squares[2][:]]
-        for b in range(last):
-            nc.scalar.activation(out=square_planes(b).rearrange("p d v -> p v d"), in_=miss[b][:], func=ACT.Square, bias=-0.5)
-            turned_sum(targets[b], planes_of(square_planes(b)))
-        nc.scalar.activation(out=square_planes(last)[:, 2:4, :].rearrange("p d v -> p v d"), in_=miss[last][:, :, 2:4],
-                             func=ACT.Square, bias=-0.5)
-        turned_sum(sum_squares[last][:], [vector_share[:, 0, :], vector_share[:, 1, :],
-                                          square_planes(last)[:, 2, :], square_planes(last)[:, 3, :]])
+        make_half_ratio(0)
+        nc.vector.scalar_tensor_tensor(out=vector_squares[:].rearrange("p d v -> p v d"),
+                                       in0=shifted[LAST][:, :, 0:SHARE], scalar=-1.0,
+                                       in1=shifted[LAST][:, :, 0:SHARE], op0=ALU.add, op1=ALU.mult)
+        make_half_ratio(1)
+        make_minus_ratio(0)
+        make_minus_ratio(1)
 
-        error = keep.tile([P, HALF], F32, name="error")
-        nc.scalar.activation(out=error[:], in_=first_pair[:], func=ACT.Copy, scale=1.0 / D)
-        turned_pair = psum.tile([P, HALF], F32, name="turned_pair", tag="turned0")
-        for b in range(2):
-            cols = slice(b * P, (b + 1) * P)
-            turned_sum(turned_pair[:, cols], [error[:, cols], ratio[:, cols]])
-        result_pair = keep.tile([P, 2, P], F32, name="result_pair")
-        nc.scalar.copy(out=result_pair[:].rearrange("p n v -> p (n v)"), in_=turned_pair[:])
-        nc.sync.dma_start(out[0:HALF, :].rearrange("(n p) v -> p n v", p=P), result_pair[:])
+        sum_pair = psum.tile([P, HALF], F32, name="sum_pair", tag="band0")
+        sum_third = psum.tile([P, P], F32, name="sum_third", tag="band2")
+        for b, acc in enumerate((sum_pair[:, 0:P], sum_pair[:, P:HALF], sum_third[:])):
+            nc.scalar.activation(out=squares[b][:].rearrange("p d v -> p v d"), in_=shifted[b][:], func=ACT.Square,
+                                 bias=-0.5)
+            turned_sum(acc, [squares[b][:, d, :] for d in range(D)])
+        nc.scalar.activation(out=squares[LAST][:, SHARE:D, :].rearrange("p d v -> p v d"),
+                             in_=shifted[LAST][:, :, SHARE:D], func=ACT.Square, bias=-0.5)
+        turned_sum(sum_last[:], [vector_squares[:, d, :] for d in range(SHARE)]
+                   + [squares[LAST][:, d, :] for d in range(SHARE, D)])
 
-        for b in (2, last):
-            cols = slice(b * P, (b + 1) * P)
-            loss = keep.tile([P, P], F32, name="loss%d" % b)
-            nc.vector.scalar_tensor_tensor(out=loss[:], in0=sum_squares[b][:], scalar=1.0 / D, in1=ratio[:, cols],
+        def turn_back(name, error_sum, cols, bank):
+            width = cols.stop - cols.start
+            loss = keep.tile([P, width], F32, name="loss_" + name)
+            nc.vector.scalar_tensor_tensor(out=loss[:], in0=error_sum[:], scalar=1.0 / D, in1=minus_ratio[:, cols],
                                            op0=ALU.mult, op1=ALU.add)
-            turned = psum.tile([P, P], F32, name="turned%d" % b, tag=("band1" if b == last else "turned1"))
-            nc.tensor.transpose(turned[:], loss[:], ident[:])
-            result = keep.tile([P, P], F32, name="result%d" % b)
-            if b == last:
-                nc.scalar.activation(out=result[:], in_=turned[:], func=ACT.Copy, bias=0.5 / D)
-            else:
-                nc.vector.tensor_copy(out=result[:], in_=turned[:])
-            nc.sync.dma_start(out[cols, :], result[:])
+            turned = psum.tile([P, width], F32, name="turned_" + name, tag=bank)
+            for first in range(0, width, P):
+                nc.tensor.transpose(turned[:, first:first + P], loss[:, first:first + P], ident[:])
+            return turned
+
+        turned = turn_back("pair", sum_pair, slice(0, HALF), "turned_pair")
+        result = keep.tile([P, 2, P], F32, name="result_pair")
+        nc.scalar.copy(out=result[:].rearrange("p n v -> p (n v)"), in_=turned[:])
+        nc.sync.dma_start(out[0:HALF, :].rearrange("(n p) v -> p n v", p=P), result[:])
+
+        turned = turn_back("third", sum_third, slice(HALF, LAST * P), "sum_overlap0")
+        result = keep.tile([P, P], F32, name="result_third")
+        nc.vector.tensor_copy(out=result[:], in_=turned[:])
+        nc.sync.dma_start(out[HALF:LAST * P, :], result[:])
+
+        turned = turn_back("last", sum_last, slice(LAST * P, V), "band1")
+        result = keep.tile([P, P], F32, name="result_last")
+        nc.scalar.activation(out=result[:], in_=turned[:], func=ACT.Copy, bias=0.25 * SHARE / D)
+        nc.sync.dma_start(out[LAST * P:V, :], result[:])

@@ -25,6 +25,7 @@ RUNS = S // D
 HALF = V // 2
 BAND_BYTES = S * 4
 GROUPED_BYTES = P * PACK * 2
+HEAD = T // 2
 SHARE = D // 2
 
 
@@ -34,43 +35,54 @@ def tile_picked_ydice_dice_p_kernel(tc, x_words, x_scales, hT, goal, offs, out):
         keep = ctx.enter_context(tc.tile_pool(name="keep", bufs=1))
         late = ctx.enter_context(tc.tile_pool(name="late", bufs=1))
         reuse = ctx.enter_context(tc.tile_pool(name="reuse", bufs=1))
+        early = ctx.enter_context(tc.tile_pool(name="early", bufs=1))
         psum = ctx.enter_context(tc.psum_pool(name="psum", bufs=1))
 
         offsets = keep.tile([P, S // 16], U16, name="offsets")
-        table_words = [keep.tile([P, T], U32, name="table_words%d" % o) for o in range(PASSES)]
-        table_scales = keep.tile([P, T], U8, name="table_scales")
+        table_scales = early.tile([P, PASSES, T], U8, name="table_scales", offset=2 * BAND_BYTES - 32)
+        table_words = [reuse.tile([P, T], U32, name="table_words0", offset=2 * BAND_BYTES - 32),
+                       keep.tile([P, T], U32, name="table_words1")]
         h_first = keep.tile([P, PACK, V], F32, name="h_first")
-        h_second = [keep.tile([P, PACK, HALF], F32, name="h_second0"),
+        h_second = [early.tile([P, PACK, HALF], F32, name="h_second0", offset=0),
                     reuse.tile([P, PACK, HALF], F32, name="h_second1", offset=0)]
-        goal_sb = [keep.tile([P, S], F32, name="goal%d" % b) for b in range(BANDS)]
+        goal_sb = [reuse.tile([P, S], F32, name="goal%d" % b, offset=(2 + b) * BAND_BYTES) for b in range(BANDS)]
         ident = keep.tile([P, P], F32, name="ident")
-        nc.gpsimd.memset(table_scales[:].bitcast(I32), 0)
+        picked_scales = keep.tile([P, PASSES, S], U8, name="picked_scales")
+        x_scale_rows = keep.tile([P, PASSES, S], U8, name="x_scale_rows", align_bytes=64)
+        x_codes = [keep.tile([P, S], U32, name="x_codes%d" % o, align_bytes=64) for o in range(PASSES)]
+        table_words_view = table_scales[:].rearrange("p o c -> p (o c)").bitcast(I32)
+        nc.gpsimd.memset(table_words_view[:, 0:768], 0)
+        nc.vector.memset(table_words_view[:, 768:1024], 0)
+        nc.vector.memset(x_scale_rows[:].rearrange("p o c -> p (o c)").bitcast(I32), 0)
 
-        def load_words(o):
-            nc.sync.dma_start(table_words[o][:].bitcast(I32), x_words[o].rearrange("p c r -> p (c r)").bitcast(I32))
+        def load_words(o, first, last):
+            words = x_words[o].rearrange("p c r -> p (c r)").bitcast(I32)
+            nc.sync.dma_start(table_words[o][:, first:last].bitcast(I32), words[:, first:last])
 
-        load_words(0)
         nc.sync.dma_start(offsets[:], offs)
-        for q in range(4):
-            nc.sync.dma_start(table_scales[32 * q:32 * q + 4 * PASSES, :].bitcast(I32),
-                              x_scales[:, 4 * q:4 * q + 4, :].bitcast(I32))
+        load_words(0, 0, HEAD)
+        nc.sync.dma_start(table_scales[0:P:8, :, :].bitcast(I32), x_scales.rearrange("o q c -> q o c").bitcast(I32))
+        load_words(0, HEAD, T)
         make_identity(nc, ident[:])
         nc.sync.dma_start(h_first[:], hT[0:PACK * P, :].rearrange("(p j) t -> p j t", j=PACK))
-        load_words(1)
+        load_words(1, 0, T)
+        for o in range(PASSES):
+            nc.vector.tensor_copy(picked_scales[:, o, :], table_scales[:, o, :].indirect(offsets[:]))
+        for r in range(4):
+            nc.sync.dma_start(x_scale_rows[r:P:32, :, :].rearrange("p o c -> p (o c)").bitcast(I32),
+                              picked_scales[8 * r:P:32, :, :].rearrange("p o c -> p (o c)").bitcast(I32))
+        nc.vector.tensor_copy(x_codes[0][:], table_words[0][:].indirect(offsets[:]))
         for pair in range(2):
             rows = hT[PACK * P:2 * PACK * P, pair * HALF:(pair + 1) * HALF]
             nc.sync.dma_start(h_second[pair][:], rows.rearrange("(p j) t -> p j t", j=PACK))
         for b in range(BANDS):
             nc.sync.dma_start(goal_sb[b][:], goal[b * P:(b + 1) * P, :])
 
-        x_codes = [keep.tile([P, S], U32, name="x_codes%d" % o, align_bytes=64) for o in range(PASSES)]
-        x_scale_rows = keep.tile([P, S], U8, name="x_scale_rows", align_bytes=64)
-
         def grouped_tile(o, b):
             name = "grouped%d_%d" % (o, b)
             if (o, b) == (PASSES - 1, LAST):
                 return reuse.tile([P, P, PACK], BF16, name=name, align_bytes=64,
-                                  offset=3 * BAND_BYTES - GROUPED_BYTES // 2)
+                                  offset=7 * BAND_BYTES - GROUPED_BYTES // 2)
             return keep.tile([P, P, PACK], BF16, name=name, align_bytes=64)
 
         grouped = [[grouped_tile(o, b) for b in range(BANDS)] for o in range(PASSES)]
@@ -95,10 +107,8 @@ def tile_picked_ydice_dice_p_kernel(tc, x_words, x_scales, hT, goal, offs, out):
                                       in_=grouped[o][b][:].rearrange("p t j -> p (t j)"))
                 nc.tensor.matmul_mx(out=scores[b][:], lhsT=h_codes[o][b][:].bitcast(FP8X4),
                                     lhsT_scale=h_scale_rows[o][b][:], rhs=x_codes[o][:].bitcast(FP8X4),
-                                    rhs_scale=x_scale_rows[4 * o:P, :], start=(o == 0), stop=(o == PASSES - 1))
+                                    rhs_scale=x_scale_rows[:, o, :], start=(o == 0), stop=(o == PASSES - 1))
 
-        nc.vector.tensor_copy(x_codes[0][:], table_words[0][:].indirect(offsets[:]))
-        nc.vector.tensor_copy(x_scale_rows[:], table_scales[:].indirect(offsets[:]))
         for pair in range(2):
             prepare_pair(0, pair)
         nc.vector.tensor_copy(x_codes[1][:], table_words[1][:].indirect(offsets[:]))
@@ -116,8 +126,8 @@ def tile_picked_ydice_dice_p_kernel(tc, x_words, x_scales, hT, goal, offs, out):
             return keep.tile(shape, F32, name="%s%d" % (name, b))
 
         tau = [band_tile("tau", b, [P, 2, S // 2], {0: 0, 1: 1}) for b in range(BANDS)]
-        overlap = [band_tile("overlap", b, [P, D, RUNS], {0: 2}) for b in range(BANDS)]
-        shifted = [band_tile("shifted", b, [P, RUNS, D], {0: 3}) for b in range(BANDS)]
+        overlap = [band_tile("overlap", b, [P, D, RUNS], {0: 6}) for b in range(BANDS)]
+        shifted = [band_tile("shifted", b, [P, RUNS, D], {0: 7}) for b in range(BANDS)]
         sum_tau = psum.tile([P, V], F32, name="sum_tau", tag="sum_tau")
         sum_overlap = [psum.tile([P, HALF], F32, name="sum_overlap%d" % pair, tag="sum_overlap%d" % pair)
                        for pair in range(2)]

@@ -26,7 +26,6 @@ HALF = V // 2
 BAND_BYTES = S * 4
 GROUPED_BYTES = P * PACK * 2
 HEAD = T // 2
-SHARE = D // 2
 
 
 def tile_picked_ydice_dice_p_kernel(tc, x_words, x_scales, hT, goal, offs, out):
@@ -55,12 +54,17 @@ def tile_picked_ydice_dice_p_kernel(tc, x_words, x_scales, hT, goal, offs, out):
         nc.vector.memset(table_words_view[:, 768:1024], 0)
         nc.vector.memset(x_scale_rows[:].rearrange("p o c -> p (o c)").bitcast(I32), 0)
 
+        zero = keep.tile([P, 1], F32, name="zero")
+        half = keep.tile([P, 1], F32, name="half")
+        nc.vector.memset(zero[:], 0.0)
+        nc.scalar.activation(out=half[:], in_=zero[:], func=ACT.Sigmoid)
+
         def load_words(o, first, last):
             words = x_words[o].rearrange("p c r -> p (c r)").bitcast(I32)
             nc.sync.dma_start(table_words[o][:, first:last].bitcast(I32), words[:, first:last])
 
-        nc.sync.dma_start(offsets[:], offs)
         load_words(0, 0, HEAD)
+        nc.sync.dma_start(offsets[:], offs)
         nc.sync.dma_start(table_scales[0:P:8, :, :].bitcast(I32), x_scales.rearrange("o q c -> q o c").bitcast(I32))
         load_words(0, HEAD, T)
         make_identity(nc, ident[:])
@@ -115,40 +119,48 @@ def tile_picked_ydice_dice_p_kernel(tc, x_words, x_scales, hT, goal, offs, out):
         for pair in range(2):
             prepare_pair(1, pair)
 
-        def turned_sum(acc, parts):
+        def turned_sum(acc, parts, opens=True, closes=True):
             for n, part in enumerate(parts):
                 nc.tensor.matmul(out=acc, lhsT=part, rhs=ident[:], is_transpose=True,
-                                 start=(n == 0), stop=(n == len(parts) - 1))
+                                 start=(opens and n == 0), stop=(closes and n == len(parts) - 1))
 
         def band_tile(name, b, shape, reused):
             if b in reused:
                 return reuse.tile(shape, F32, name="%s%d" % (name, b), offset=reused[b] * BAND_BYTES)
             return keep.tile(shape, F32, name="%s%d" % (name, b))
 
-        tau = [band_tile("tau", b, [P, 2, S // 2], {0: 0, 1: 1}) for b in range(BANDS)]
+        score = [band_tile("score", b, [P, D, RUNS], {0: 0, 1: 1}) for b in range(BANDS)]
         overlap = [band_tile("overlap", b, [P, D, RUNS], {0: 6}) for b in range(BANDS)]
-        shifted = [band_tile("shifted", b, [P, RUNS, D], {0: 7}) for b in range(BANDS)]
-        sum_tau = psum.tile([P, V], F32, name="sum_tau", tag="sum_tau")
+        missing = [band_tile("missing", b, [P, D, RUNS], {0: 7}) for b in range(BANDS)]
+        sum_score = psum.tile([P, V], F32, name="sum_score", tag="sum_score")
         sum_overlap = [psum.tile([P, HALF], F32, name="sum_overlap%d" % pair, tag="sum_overlap%d" % pair)
                        for pair in range(2)]
-        for b in range(BANDS):
-            nc.scalar.activation(out=tau[b][:], in_=scores[b][:].rearrange("p (w l) -> p l w", l=2), func=ACT.Tanh,
-                                 scale=0.5)
-            turned_sum(sum_tau[:, b * P:(b + 1) * P], [tau[b][:, l, h::2] for l in range(2) for h in range(2)])
 
-        def in_point_order(b):
-            return tau[b][:].rearrange("p l w -> p w l"), goal_sb[b][:].rearrange("p (w l) -> p w l", l=2)
+        def planes(tile):
+            return [tile[:, d, :] for d in range(D)]
+
+        for b in range(BANDS):
+            nc.scalar.activation(out=score[b][:], in_=scores[b][:].rearrange("p (v d) -> p d v", d=D),
+                                 func=ACT.Sigmoid)
+            turned_sum(sum_score[:, b * P:(b + 1) * P], planes(score[b]))
+
+        def with_goal(result, b, op):
+            walk = "p d (c i) -> p c d i"
+            nc.vector.tensor_tensor(out=result[:].rearrange(walk, i=2), in0=score[b][:].rearrange(walk, i=2),
+                                    in1=goal_sb[b][:].rearrange("p (c i d) -> p c d i", i=2, d=D), op=op)
 
         def make_overlap(b):
-            tau_points, goal_points = in_point_order(b)
-            nc.vector.scalar_tensor_tensor(out=overlap[b][:].rearrange("p d v -> p v d"), in0=tau_points, scalar=1.0,
-                                           in1=goal_points, op0=ALU.add, op1=ALU.mult)
-            turned_sum(sum_overlap[b // 2][:, (b % 2) * P:(b % 2 + 1) * P], [overlap[b][:, d, :] for d in range(D)])
+            with_goal(overlap[b], b, ALU.mult)
+            turned_sum(sum_overlap[b // 2][:, (b % 2) * P:(b % 2 + 1) * P], planes(overlap[b]))
+
+        turned_missing = {}
 
         def make_shifted(b):
-            tau_points, goal_points = in_point_order(b)
-            nc.vector.scalar_tensor_tensor(out=shifted[b][:].rearrange("p v (h l) -> p (v h) l", l=2), in0=tau_points,
-                                           scalar=-0.5, in1=goal_points, op0=ALU.mult, op1=ALU.add)
+            with_goal(missing[b], b, ALU.subtract)
+            if b >= 1:
+                turned_missing[b] = psum.tile([P, D, P], F32, name="turned_missing%d" % b, tag="band%d" % b)
+                for d in range(D):
+                    nc.tensor.transpose(turned_missing[b][:, d, :], missing[b][:, d, :], ident[:])
 
         make_overlap(0)
         make_shifted(0)
@@ -159,66 +171,47 @@ def tile_picked_ydice_dice_p_kernel(tc, x_words, x_scales, hT, goal, offs, out):
 
         root = keep.tile([P, V], F32, name="root")
         six = late.tile([P, LAST * S], F32, name="six", offset=0)
-        nc.gpsimd.memset(six[:, 0:1], 6.0)
-        nc.scalar.activation(out=root[:], in_=sum_tau[:], func=ACT.Abs_reciprocal_sqrt, scale=0.5, bias=six[:, 0:1])
+        nc.gpsimd.memset(six[:, 0:1], 4.0)
+        nc.scalar.activation(out=root[:], in_=sum_score[:], func=ACT.Abs_reciprocal_sqrt, bias=six[:, 0:1])
         squares = [keep.tile([P, D, RUNS], F32, name="squares0")]
         squares.extend(late.tile([P, D, RUNS], F32, name="squares%d" % b, offset=(b - 1) * BAND_BYTES)
                        for b in range(1, BANDS))
-        vector_squares = keep.tile([P, SHARE, RUNS], F32, name="vector_squares")
-        sum_last = psum.tile([P, P], F32, name="sum_last", tag="band%d" % LAST)
         half_ratio = keep.tile([P, V], F32, name="half_ratio")
         minus_ratio = keep.tile([P, V], F32, name="minus_ratio")
 
         def make_half_ratio(pair):
             cols = slice(pair * HALF, (pair + 1) * HALF)
-            nc.vector.scalar_tensor_tensor(out=half_ratio[:, cols], in0=sum_overlap[pair][:], scalar=1.0,
+            nc.vector.scalar_tensor_tensor(out=half_ratio[:, cols], in0=sum_overlap[pair][:], scalar=0.5,
                                            in1=root[:, cols], op0=ALU.add, op1=ALU.mult)
 
         def make_minus_ratio(pair):
             cols = slice(pair * HALF, (pair + 1) * HALF)
-            nc.vector.scalar_tensor_tensor(out=minus_ratio[:, cols], in0=half_ratio[:, cols], scalar=-1.0,
+            nc.vector.scalar_tensor_tensor(out=minus_ratio[:, cols], in0=half_ratio[:, cols], scalar=-2.0,
                                            in1=root[:, cols], op0=ALU.mult, op1=ALU.mult)
 
         make_half_ratio(0)
-        nc.vector.scalar_tensor_tensor(out=vector_squares[:].rearrange("p d v -> p v d"),
-                                       in0=shifted[LAST][:, :, 0:SHARE], scalar=-1.0,
-                                       in1=shifted[LAST][:, :, 0:SHARE], op0=ALU.add, op1=ALU.mult)
         make_half_ratio(1)
         make_minus_ratio(0)
         make_minus_ratio(1)
 
-        sum_pair = psum.tile([P, HALF], F32, name="sum_pair", tag="band0")
-        sum_third = psum.tile([P, P], F32, name="sum_third", tag="band2")
-        for b, acc in enumerate((sum_pair[:, 0:P], sum_pair[:, P:HALF], sum_third[:])):
-            nc.scalar.activation(out=squares[b][:].rearrange("p d v -> p v d"), in_=shifted[b][:], func=ACT.Square,
-                                 bias=-0.5)
-            turned_sum(acc, [squares[b][:, d, :] for d in range(D)])
-        nc.scalar.activation(out=squares[LAST][:, SHARE:D, :].rearrange("p d v -> p v d"),
-                             in_=shifted[LAST][:, :, SHARE:D], func=ACT.Square, bias=-0.5)
-        turned_sum(sum_last[:], [vector_squares[:, d, :] for d in range(SHARE)]
-                   + [squares[LAST][:, d, :] for d in range(SHARE, D)])
-
-        def turn_back(name, error_sum, cols, bank):
-            width = cols.stop - cols.start
-            loss = keep.tile([P, width], F32, name="loss_" + name)
-            nc.vector.scalar_tensor_tensor(out=loss[:], in0=error_sum[:], scalar=1.0 / D, in1=minus_ratio[:, cols],
-                                           op0=ALU.mult, op1=ALU.add)
-            turned = psum.tile([P, width], F32, name="turned_" + name, tag=bank)
-            for first in range(0, width, P):
-                nc.tensor.transpose(turned[:, first:first + P], loss[:, first:first + P], ident[:])
-            return turned
-
-        turned = turn_back("pair", sum_pair, slice(0, HALF), "turned_pair")
-        result = keep.tile([P, 2, P], F32, name="result_pair")
-        nc.scalar.copy(out=result[:].rearrange("p n v -> p (n v)"), in_=turned[:])
-        nc.sync.dma_start(out[0:HALF, :].rearrange("(n p) v -> p n v", p=P), result[:])
-
-        turned = turn_back("third", sum_third, slice(HALF, LAST * P), "sum_overlap0")
-        result = keep.tile([P, P], F32, name="result_third")
-        nc.vector.tensor_copy(out=result[:], in_=turned[:])
-        nc.sync.dma_start(out[HALF:LAST * P, :], result[:])
-
-        turned = turn_back("last", sum_last, slice(LAST * P, V), "band1")
-        result = keep.tile([P, P], F32, name="result_last")
-        nc.scalar.activation(out=result[:], in_=turned[:], func=ACT.Copy, bias=0.25 * SHARE / D)
-        nc.sync.dma_start(out[LAST * P:V, :], result[:])
+        sum_first = psum.tile([P, P], F32, name="sum_first", tag="band0")
+        nc.scalar.activation(out=squares[0][:], in_=missing[0][:], func=ACT.Square)
+        turned_sum(sum_first[:], [squares[0][:, d, :] for d in range(D)])
+        loss = keep.tile([P, P], F32, name="loss")
+        nc.vector.scalar_tensor_tensor(out=loss[:], in0=sum_first[:], scalar=1.0 / D, in1=minus_ratio[:, 0:P],
+                                       op0=ALU.mult, op1=ALU.add)
+        finals = [psum.tile([P, P], F32, name="final0", tag="final0")]
+        for b, bank in ((1, "sum_score"), (2, "sum_overlap0"), (3, "sum_overlap1")):
+            nc.scalar.activation(out=squares[b][:], in_=turned_missing[b][:], func=ACT.Square,
+                                 scale=half[:, 0:1])
+            finals.append(psum.tile([P, P], F32, name="final%d" % b, tag=bank))
+            turned_sum(finals[b][:], [squares[b][:, d, :] for d in range(D)], closes=False)
+        turned_sum(finals[1][:], [minus_ratio[:, P:HALF]], opens=False)
+        nc.tensor.transpose(finals[0][:], loss[:], ident[:])
+        for b in (2, 3):
+            turned_sum(finals[b][:], [minus_ratio[:, b * P:(b + 1) * P]], opens=False)
+        for pair in range(2):
+            result = keep.tile([P, 2, P], F32, name="result%d" % pair)
+            nc.vector.tensor_copy(out=result[:, 1, :], in_=finals[2 * pair + 1][:])
+            nc.scalar.copy(out=result[:, 0, :], in_=finals[2 * pair][:])
+            nc.sync.dma_start(out[pair * HALF:(pair + 1) * HALF, :].rearrange("(n p) v -> p n v", p=P), result[:])

@@ -54,7 +54,7 @@ def tile_picked_ydice_dice_p_kernel(tc, x_words, x_scales, hT, goal, offs, out):
         nc.vector.memset(table_words_view[:, 768:1024], 0)
         nc.vector.memset(x_scale_rows[:].rearrange("p o c -> p (o c)").bitcast(I32), 0)
 
-        zero = keep.tile([P, 1], F32, name="zero")
+        zero = late.tile([P, 1], F32, name="zero", offset=LAST * BAND_BYTES)
         half = keep.tile([P, 1], F32, name="half")
         nc.vector.memset(zero[:], 0.0)
         nc.scalar.activation(out=half[:], in_=zero[:], func=ACT.Sigmoid)
@@ -105,7 +105,11 @@ def tile_picked_ydice_dice_p_kernel(tc, x_words, x_scales, hT, goal, offs, out):
             even, odd = 2 * pair, 2 * pair + 1
             nc.vector.tensor_copy(out=grouped[o][even][:].rearrange("p (c i) j -> p c j i", i=4),
                                   in_=raw_band(o, even).rearrange("p j (c i) -> p c j i", i=4))
-            nc.scalar.copy(out=grouped[o][odd][:], in_=raw_band(o, odd).rearrange("p j t -> p t j"))
+            if (o, odd) == (PASSES - 1, LAST):
+                nc.vector.tensor_copy(out=grouped[o][odd][:].rearrange("p (c i) j -> p c j i", i=4),
+                                      in_=raw_band(o, odd).rearrange("p j (c i) -> p c j i", i=4))
+            else:
+                nc.scalar.copy(out=grouped[o][odd][:], in_=raw_band(o, odd).rearrange("p j t -> p t j"))
             for b in (even, odd):
                 nc.vector.quantize_mx(out=h_codes[o][b][:].bitcast(FP8X4), scales=h_scale_rows[o][b][:],
                                       in_=grouped[o][b][:].rearrange("p t j -> p (t j)"))
@@ -129,7 +133,7 @@ def tile_picked_ydice_dice_p_kernel(tc, x_words, x_scales, hT, goal, offs, out):
                 return reuse.tile(shape, F32, name="%s%d" % (name, b), offset=reused[b] * BAND_BYTES)
             return keep.tile(shape, F32, name="%s%d" % (name, b))
 
-        score = [band_tile("score", b, [P, D, RUNS], {0: 0, 1: 1}) for b in range(BANDS)]
+        score = [band_tile("score", b, [P, D, RUNS], {1: 1}) for b in range(BANDS)]
         overlap = [band_tile("overlap", b, [P, D, RUNS], {0: 6}) for b in range(BANDS)]
         missing = [band_tile("missing", b, [P, D, RUNS], {0: 7}) for b in range(BANDS)]
         sum_score = psum.tile([P, V], F32, name="sum_score", tag="sum_score")
@@ -141,7 +145,7 @@ def tile_picked_ydice_dice_p_kernel(tc, x_words, x_scales, hT, goal, offs, out):
 
         for b in range(BANDS):
             nc.scalar.activation(out=score[b][:], in_=scores[b][:].rearrange("p (v d) -> p d v", d=D),
-                                 func=ACT.Sigmoid)
+                                 func=ACT.Sigmoid, bias=zero[:])
             turned_sum(sum_score[:, b * P:(b + 1) * P], planes(score[b]))
 
         def with_goal(result, b, op):
@@ -173,7 +177,7 @@ def tile_picked_ydice_dice_p_kernel(tc, x_words, x_scales, hT, goal, offs, out):
         six = late.tile([P, LAST * S], F32, name="six", offset=0)
         nc.gpsimd.memset(six[:, 0:1], 4.0)
         nc.scalar.activation(out=root[:], in_=sum_score[:], func=ACT.Abs_reciprocal_sqrt, bias=six[:, 0:1])
-        squares = [keep.tile([P, D, RUNS], F32, name="squares0")]
+        squares = [late.tile([P, D, RUNS], F32, name="squares0", offset=LAST * BAND_BYTES)]
         squares.extend(late.tile([P, D, RUNS], F32, name="squares%d" % b, offset=(b - 1) * BAND_BYTES)
                        for b in range(1, BANDS))
         half_ratio = keep.tile([P, V], F32, name="half_ratio")
@@ -205,11 +209,12 @@ def tile_picked_ydice_dice_p_kernel(tc, x_words, x_scales, hT, goal, offs, out):
             nc.scalar.activation(out=squares[b][:], in_=turned_missing[b][:], func=ACT.Square,
                                  scale=half[:, 0:1])
             finals.append(psum.tile([P, P], F32, name="final%d" % b, tag=bank))
-            turned_sum(finals[b][:], [squares[b][:, d, :] for d in range(D)], closes=False)
+            if b < LAST:
+                turned_sum(finals[b][:], planes(squares[b]), closes=False)
         turned_sum(finals[1][:], [minus_ratio[:, P:HALF]], opens=False)
+        turned_sum(finals[2][:], [minus_ratio[:, HALF:LAST * P]], opens=False)
         nc.tensor.transpose(finals[0][:], loss[:], ident[:])
-        for b in (2, 3):
-            turned_sum(finals[b][:], [minus_ratio[:, b * P:(b + 1) * P]], opens=False)
+        turned_sum(finals[LAST][:], [minus_ratio[:, LAST * P:V]] + planes(squares[LAST]))
         for pair in range(2):
             result = keep.tile([P, 2, P], F32, name="result%d" % pair)
             nc.vector.tensor_copy(out=result[:, 1, :], in_=finals[2 * pair + 1][:])

@@ -166,10 +166,17 @@ def tile_picked_ydice_dice_p_kernel(tc, x_words, x_scales, hT, goal, offs, out):
                 for d in range(D):
                     nc.tensor.transpose(turned_missing[b][:, d, :], missing[b][:, d, :], ident[:])
 
+        def warm_up(bank):
+            unread = psum.tile([P, S], F32, name="unread_" + bank, tag=bank)
+            nc.tensor.matmul_mx(out=unread[:], lhsT=h_codes[0][0][:].bitcast(FP8X4), lhsT_scale=h_scale_rows[0][0][:],
+                                rhs=x_codes[0][:].bitcast(FP8X4), rhs_scale=x_scale_rows[:, 0, :], start=True,
+                                stop=True)
+
         make_overlap(0)
         make_shifted(0)
         for b in range(1, BANDS):
             make_overlap(b)
+        warm_up("band3")
         for b in range(1, BANDS):
             make_shifted(b)
 
@@ -193,6 +200,7 @@ def tile_picked_ydice_dice_p_kernel(tc, x_words, x_scales, hT, goal, offs, out):
             nc.vector.scalar_tensor_tensor(out=minus_ratio[:, cols], in0=half_ratio[:, cols], scalar=-2.0,
                                            in1=root[:, cols], op0=ALU.mult, op1=ALU.mult)
 
+        warm_up("sum_score")
         make_half_ratio(0)
         make_half_ratio(1)
         make_minus_ratio(0)

@@ -137,7 +137,7 @@ def tile_picked_ydice_dice_p_kernel(tc, x_words, x_scales, hT, goal, offs, out):
         overlap = [band_tile("overlap", b, [P, D, RUNS], {0: 6}) for b in range(BANDS)]
         missing = [band_tile("missing", b, [P, D, RUNS], {0: 7}) for b in range(BANDS)]
         sum_score = psum.tile([P, V], F32, name="sum_score", tag="sum_score")
-        sum_overlap = [psum.tile([P, HALF], F32, name="sum_overlap%d" % pair, tag="sum_overlap%d" % pair)
+        sum_overlap = [psum.tile([P, V], F32, name="sum_overlap%d" % pair, tag="sum_overlap%d" % pair)
                        for pair in range(2)]
 
         def planes(tile):
@@ -166,18 +166,15 @@ def tile_picked_ydice_dice_p_kernel(tc, x_words, x_scales, hT, goal, offs, out):
                 for d in range(D):
                     nc.tensor.transpose(turned_missing[b][:, d, :], missing[b][:, d, :], ident[:])
 
-        def warm_up(bank):
-            unread = psum.tile([P, S], F32, name="unread_" + bank, tag=bank)
-            nc.tensor.matmul_mx(out=unread[:], lhsT=h_codes[0][0][:].bitcast(FP8X4), lhsT_scale=h_scale_rows[0][0][:],
-                                rhs=x_codes[0][:].bitcast(FP8X4), rhs_scale=x_scale_rows[:, 0, :], start=True,
-                                stop=True)
+        def warm_up(unread):
+            nc.tensor.matmul_mx(out=unread, lhsT=h_codes[0][0][:].bitcast(FP8X4), lhsT_scale=h_scale_rows[0][0][:],
+                                rhs=x_codes[0][:, 0:HALF].bitcast(FP8X4), rhs_scale=x_scale_rows[:, 0, 0:HALF],
+                                start=True, stop=True)
 
-        make_overlap(0)
-        make_shifted(0)
-        for b in range(1, BANDS):
+        for b in range(BANDS):
             make_overlap(b)
-        warm_up("band3")
-        for b in range(1, BANDS):
+            if b > 0:
+                warm_up(sum_overlap[b // 2][:, HALF:V])
             make_shifted(b)
 
         root = keep.tile([P, V], F32, name="root")
@@ -192,7 +189,7 @@ def tile_picked_ydice_dice_p_kernel(tc, x_words, x_scales, hT, goal, offs, out):
 
         def make_half_ratio(pair):
             cols = slice(pair * HALF, (pair + 1) * HALF)
-            nc.vector.scalar_tensor_tensor(out=half_ratio[:, cols], in0=sum_overlap[pair][:], scalar=0.5,
+            nc.vector.scalar_tensor_tensor(out=half_ratio[:, cols], in0=sum_overlap[pair][:, 0:HALF], scalar=0.5,
                                            in1=root[:, cols], op0=ALU.add, op1=ALU.mult)
 
         def make_minus_ratio(pair):
@@ -200,7 +197,7 @@ def tile_picked_ydice_dice_p_kernel(tc, x_words, x_scales, hT, goal, offs, out):
             nc.vector.scalar_tensor_tensor(out=minus_ratio[:, cols], in0=half_ratio[:, cols], scalar=-2.0,
                                            in1=root[:, cols], op0=ALU.mult, op1=ALU.mult)
 
-        warm_up("sum_score")
+        warm_up(psum.tile([P, HALF], F32, name="unread", tag="sum_score")[:])
         make_half_ratio(0)
         make_half_ratio(1)
         make_minus_ratio(0)

@@ -42,11 +42,14 @@ def tile_picked_ydice_dice_p_kernel(tc, x_words, x_scales, hT, goal, offs, out):
         table_words = [reuse.tile([P, T], U32, name="table_words0", offset=2 * BAND_BYTES - 32),
                        keep.tile([P, T], U32, name="table_words1")]
         h_first = keep.tile([P, PACK, V], F32, name="h_first")
-        h_second = [early.tile([P, PACK, HALF], F32, name="h_second0", offset=0),
-                    reuse.tile([P, PACK, HALF], F32, name="h_second1", offset=0)]
-        goal_sb = [reuse.tile([P, S], F32, name="goal%d" % b, offset=(2 + b) * BAND_BYTES) for b in range(BANDS)]
+        h_second = [early.tile([P, PACK, P], F32, name="h_second0", offset=BAND_BYTES),
+                    early.tile([P, PACK, P], F32, name="h_second1", offset=2 * BAND_BYTES),
+                    reuse.tile([P, PACK, P], F32, name="h_second2", offset=BAND_BYTES),
+                    reuse.tile([P, PACK, P], F32, name="h_second3", offset=2 * BAND_BYTES)]
+        goal_sb = [reuse.tile([P, S], F32, name="goal%d" % b, offset=(3 + b) * BAND_BYTES) for b in range(LAST)]
+        goal_sb.append(early.tile([P, S], F32, name="goal%d" % LAST, offset=4 * BAND_BYTES))
         ident = keep.tile([P, P], F32, name="ident")
-        picked_scales = keep.tile([P, PASSES, S], U8, name="picked_scales")
+        picked_scales = early.tile([P, PASSES, S], U8, name="picked_scales", offset=4 * BAND_BYTES)
         x_scale_rows = keep.tile([P, PASSES, S], U8, name="x_scale_rows", align_bytes=64)
         x_codes = [keep.tile([P, S], U32, name="x_codes%d" % o, align_bytes=64) for o in range(PASSES)]
         table_words_view = table_scales[:].rearrange("p o c -> p (o c)").bitcast(I32)
@@ -76,9 +79,9 @@ def tile_picked_ydice_dice_p_kernel(tc, x_words, x_scales, hT, goal, offs, out):
             nc.sync.dma_start(x_scale_rows[r:P:32, :, :].rearrange("p o c -> p (o c)").bitcast(I32),
                               picked_scales[8 * r:P:32, :, :].rearrange("p o c -> p (o c)").bitcast(I32))
         nc.vector.tensor_copy(x_codes[0][:], table_words[0][:].indirect(offsets[:]))
-        for pair in range(2):
-            rows = hT[PACK * P:2 * PACK * P, pair * HALF:(pair + 1) * HALF]
-            nc.sync.dma_start(h_second[pair][:], rows.rearrange("(p j) t -> p j t", j=PACK))
+        for b in range(BANDS):
+            rows = hT[PACK * P:2 * PACK * P, b * P:(b + 1) * P]
+            nc.sync.dma_start(h_second[b][:], rows.rearrange("(p j) t -> p j t", j=PACK))
         for b in range(BANDS):
             nc.sync.dma_start(goal_sb[b][:], goal[b * P:(b + 1) * P, :])
 
@@ -99,29 +102,32 @@ def tile_picked_ydice_dice_p_kernel(tc, x_words, x_scales, hT, goal, offs, out):
         def raw_band(o, b):
             if o == 0:
                 return h_first[:, :, b * P:(b + 1) * P]
-            return h_second[b // 2][:, :, (b % 2) * P:(b % 2 + 1) * P]
+            return h_second[b][:]
 
-        def prepare_pair(o, pair):
-            even, odd = 2 * pair, 2 * pair + 1
-            nc.vector.tensor_copy(out=grouped[o][even][:].rearrange("p (c i) j -> p c j i", i=4),
-                                  in_=raw_band(o, even).rearrange("p j (c i) -> p c j i", i=4))
-            if (o, odd) == (PASSES - 1, LAST):
-                nc.vector.tensor_copy(out=grouped[o][odd][:].rearrange("p (c i) j -> p c j i", i=4),
-                                      in_=raw_band(o, odd).rearrange("p j (c i) -> p c j i", i=4))
+        def prepare(o, b, on_vector):
+            if on_vector:
+                nc.vector.tensor_copy(out=grouped[o][b][:].rearrange("p (c i) j -> p c j i", i=4),
+                                      in_=raw_band(o, b).rearrange("p j (c i) -> p c j i", i=4))
             else:
-                nc.scalar.copy(out=grouped[o][odd][:], in_=raw_band(o, odd).rearrange("p j t -> p t j"))
-            for b in (even, odd):
-                nc.vector.quantize_mx(out=h_codes[o][b][:].bitcast(FP8X4), scales=h_scale_rows[o][b][:],
-                                      in_=grouped[o][b][:].rearrange("p t j -> p (t j)"))
-                nc.tensor.matmul_mx(out=scores[b][:], lhsT=h_codes[o][b][:].bitcast(FP8X4),
-                                    lhsT_scale=h_scale_rows[o][b][:], rhs=x_codes[o][:].bitcast(FP8X4),
-                                    rhs_scale=x_scale_rows[:, o, :], start=(o == 0), stop=(o == PASSES - 1))
+                nc.scalar.copy(out=grouped[o][b][:], in_=raw_band(o, b).rearrange("p j t -> p t j"))
+            nc.vector.quantize_mx(out=h_codes[o][b][:].bitcast(FP8X4), scales=h_scale_rows[o][b][:],
+                                  in_=grouped[o][b][:].rearrange("p t j -> p (t j)"))
 
-        for pair in range(2):
-            prepare_pair(0, pair)
+        def product(o, b, opens):
+            nc.tensor.matmul_mx(out=scores[b][:], lhsT=h_codes[o][b][:].bitcast(FP8X4),
+                                lhsT_scale=h_scale_rows[o][b][:], rhs=x_codes[o][:].bitcast(FP8X4),
+                                rhs_scale=x_scale_rows[:, o, :], start=opens, stop=not opens)
+
+        for b in range(BANDS):
+            prepare(0, b, b % 2 == 0)
+        for b in range(2):
+            product(0, b, True)
         nc.vector.tensor_copy(x_codes[1][:], table_words[1][:].indirect(offsets[:]))
-        for pair in range(2):
-            prepare_pair(1, pair)
+        for b in range(BANDS):
+            prepare(1, b, b >= 2)
+            product(1, b, b >= 2)
+            if b >= 2:
+                product(0, b, False)
 
         def turned_sum(acc, parts, opens=True, closes=True):
             for n, part in enumerate(parts):
@@ -133,10 +139,10 @@ def tile_picked_ydice_dice_p_kernel(tc, x_words, x_scales, hT, goal, offs, out):
                 return reuse.tile(shape, F32, name="%s%d" % (name, b), offset=reused[b] * BAND_BYTES)
             return keep.tile(shape, F32, name="%s%d" % (name, b))
 
-        score = [band_tile("score", b, [P, D, RUNS], {1: 1}) for b in range(BANDS)]
+        score = [band_tile("score", b, [P, D, RUNS], {}) for b in range(BANDS)]
         overlap = [band_tile("overlap", b, [P, D, RUNS], {0: 6}) for b in range(BANDS)]
         missing = [band_tile("missing", b, [P, D, RUNS], {0: 7}) for b in range(BANDS)]
-        sum_score = psum.tile([P, V], F32, name="sum_score", tag="sum_score")
+        sum_score = psum.tile([P, V], F32, name="sum_score", tag="band2")
         sum_overlap = [psum.tile([P, V], F32, name="sum_overlap%d" % pair, tag="sum_overlap%d" % pair)
                        for pair in range(2)]
 
@@ -146,6 +152,7 @@ def tile_picked_ydice_dice_p_kernel(tc, x_words, x_scales, hT, goal, offs, out):
         for b in range(BANDS):
             nc.scalar.activation(out=score[b][:], in_=scores[b][:].rearrange("p (v d) -> p d v", d=D),
                                  func=ACT.Sigmoid, bias=zero[:])
+        for b in range(BANDS):
             turned_sum(sum_score[:, b * P:(b + 1) * P], planes(score[b]))
 
         def with_goal(result, b, op):
@@ -162,7 +169,7 @@ def tile_picked_ydice_dice_p_kernel(tc, x_words, x_scales, hT, goal, offs, out):
         def make_shifted(b):
             with_goal(missing[b], b, ALU.subtract)
             if b >= 1:
-                turned_missing[b] = psum.tile([P, D, P], F32, name="turned_missing%d" % b, tag="band%d" % b)
+                turned_missing[b] = psum.tile([P, D, P], F32, name="turned_missing%d" % b, tag=("band1", "spare", "band3")[b - 1])
                 for d in range(D):
                     nc.tensor.transpose(turned_missing[b][:, d, :], missing[b][:, d, :], ident[:])
 
@@ -197,7 +204,7 @@ def tile_picked_ydice_dice_p_kernel(tc, x_words, x_scales, hT, goal, offs, out):
             nc.vector.scalar_tensor_tensor(out=minus_ratio[:, cols], in0=half_ratio[:, cols], scalar=-2.0,
                                            in1=root[:, cols], op0=ALU.mult, op1=ALU.mult)
 
-        warm_up(psum.tile([P, HALF], F32, name="unread", tag="sum_score")[:])
+        warm_up(psum.tile([P, HALF], F32, name="unread", tag="band2")[:])
         make_half_ratio(0)
         make_half_ratio(1)
         make_minus_ratio(0)
@@ -210,7 +217,7 @@ def tile_picked_ydice_dice_p_kernel(tc, x_words, x_scales, hT, goal, offs, out):
         nc.vector.scalar_tensor_tensor(out=loss[:], in0=sum_first[:], scalar=1.0 / D, in1=minus_ratio[:, 0:P],
                                        op0=ALU.mult, op1=ALU.add)
         finals = [psum.tile([P, P], F32, name="final0", tag="final0")]
-        for b, bank in ((1, "sum_score"), (2, "sum_overlap0"), (3, "sum_overlap1")):
+        for b, bank in ((1, "band2"), (2, "sum_overlap0"), (3, "sum_overlap1")):
             nc.scalar.activation(out=squares[b][:], in_=turned_missing[b][:], func=ACT.Square,
                                  scale=half[:, 0:1])
             finals.append(psum.tile([P, P], F32, name="final%d" % b, tag=bank))

@@ -42,8 +42,7 @@ def tile_picked_ydice_dice_p_kernel(tc, x_words, x_scales, hT, goal, offs, out):
         table_words = [reuse.tile([P, T], U32, name="table_words0", offset=2 * BAND_BYTES - 32),
                        keep.tile([P, T], U32, name="table_words1")]
         h_first = keep.tile([P, PACK, V], F32, name="h_first")
-        h_second = [early.tile([P, PACK, P], F32, name="h_second0", offset=BAND_BYTES),
-                    early.tile([P, PACK, P], F32, name="h_second1", offset=2 * BAND_BYTES),
+        h_second = [early.tile([P, PACK, HALF], F32, name="h_second0", offset=0),
                     reuse.tile([P, PACK, P], F32, name="h_second2", offset=BAND_BYTES),
                     reuse.tile([P, PACK, P], F32, name="h_second3", offset=2 * BAND_BYTES)]
         goal_sb = [reuse.tile([P, S], F32, name="goal%d" % b, offset=(3 + b) * BAND_BYTES) for b in range(LAST)]
@@ -79,9 +78,9 @@ def tile_picked_ydice_dice_p_kernel(tc, x_words, x_scales, hT, goal, offs, out):
             nc.sync.dma_start(x_scale_rows[r:P:32, :, :].rearrange("p o c -> p (o c)").bitcast(I32),
                               picked_scales[8 * r:P:32, :, :].rearrange("p o c -> p (o c)").bitcast(I32))
         nc.vector.tensor_copy(x_codes[0][:], table_words[0][:].indirect(offsets[:]))
-        for b in range(BANDS):
-            rows = hT[PACK * P:2 * PACK * P, b * P:(b + 1) * P]
-            nc.sync.dma_start(h_second[b][:], rows.rearrange("(p j) t -> p j t", j=PACK))
+        for piece, (first, last) in zip(h_second, ((0, HALF), (HALF, LAST * P), (LAST * P, V))):
+            rows = hT[PACK * P:2 * PACK * P, first:last]
+            nc.sync.dma_start(piece[:], rows.rearrange("(p j) t -> p j t", j=PACK))
         for b in range(BANDS):
             nc.sync.dma_start(goal_sb[b][:], goal[b * P:(b + 1) * P, :])
 
@@ -102,7 +101,9 @@ def tile_picked_ydice_dice_p_kernel(tc, x_words, x_scales, hT, goal, offs, out):
         def raw_band(o, b):
             if o == 0:
                 return h_first[:, :, b * P:(b + 1) * P]
-            return h_second[b][:]
+            if b < 2:
+                return h_second[0][:, :, b * P:(b + 1) * P]
+            return h_second[b - 1][:]
 
         def prepare(o, b, on_vector):
             if on_vector:
@@ -120,14 +121,13 @@ def tile_picked_ydice_dice_p_kernel(tc, x_words, x_scales, hT, goal, offs, out):
 
         for b in range(BANDS):
             prepare(0, b, b % 2 == 0)
-        for b in range(2):
+        for b in range(LAST):
             product(0, b, True)
         nc.vector.tensor_copy(x_codes[1][:], table_words[1][:].indirect(offsets[:]))
         for b in range(BANDS):
-            prepare(1, b, b >= 2)
-            product(1, b, b >= 2)
-            if b >= 2:
-                product(0, b, False)
+            prepare(1, b, b != 1)
+            product(1, b, b == LAST)
+        product(0, LAST, False)
 
         def turned_sum(acc, parts, opens=True, closes=True):
             for n, part in enumerate(parts):
@@ -143,7 +143,7 @@ def tile_picked_ydice_dice_p_kernel(tc, x_words, x_scales, hT, goal, offs, out):
         overlap = [band_tile("overlap", b, [P, D, RUNS], {0: 6}) for b in range(BANDS)]
         missing = [band_tile("missing", b, [P, D, RUNS], {0: 7}) for b in range(BANDS)]
         sum_score = psum.tile([P, V], F32, name="sum_score", tag="band2")
-        sum_overlap = [psum.tile([P, V], F32, name="sum_overlap%d" % pair, tag="sum_overlap%d" % pair)
+        sum_overlap = [psum.tile([P, (pair + 1) * HALF], F32, name="sum_overlap%d" % pair, tag="sum_overlap%d" % pair)
                        for pair in range(2)]
 
         def planes(tile):
@@ -178,10 +178,14 @@ def tile_picked_ydice_dice_p_kernel(tc, x_words, x_scales, hT, goal, offs, out):
                                 rhs=x_codes[0][:, 0:HALF].bitcast(FP8X4), rhs_scale=x_scale_rows[:, 0, 0:HALF],
                                 start=True, stop=True)
 
-        for b in range(BANDS):
+        for b in range(2):
             make_overlap(b)
-            if b > 0:
-                warm_up(sum_overlap[b // 2][:, HALF:V])
+            make_shifted(b)
+        for b in range(2, BANDS):
+            make_overlap(b)
+            for repeat in range(2):
+                warm_up(sum_overlap[1][:, HALF:V])
+        for b in range(2, BANDS):
             make_shifted(b)
 
         root = keep.tile([P, V], F32, name="root")
@@ -204,7 +208,6 @@ def tile_picked_ydice_dice_p_kernel(tc, x_words, x_scales, hT, goal, offs, out):
             nc.vector.scalar_tensor_tensor(out=minus_ratio[:, cols], in0=half_ratio[:, cols], scalar=-2.0,
                                            in1=root[:, cols], op0=ALU.mult, op1=ALU.mult)
 
-        warm_up(psum.tile([P, HALF], F32, name="unread", tag="band2")[:])
         make_half_ratio(0)
         make_half_ratio(1)
         make_minus_ratio(0)
@@ -227,8 +230,13 @@ def tile_picked_ydice_dice_p_kernel(tc, x_words, x_scales, hT, goal, offs, out):
         turned_sum(finals[2][:], [minus_ratio[:, HALF:LAST * P]], opens=False)
         nc.tensor.transpose(finals[0][:], loss[:], ident[:])
         turned_sum(finals[LAST][:], [minus_ratio[:, LAST * P:V]] + planes(squares[LAST]))
-        for pair in range(2):
-            result = keep.tile([P, 2, P], F32, name="result%d" % pair)
-            nc.vector.tensor_copy(out=result[:, 1, :], in_=finals[2 * pair + 1][:])
-            nc.scalar.copy(out=result[:, 0, :], in_=finals[2 * pair][:])
-            nc.sync.dma_start(out[pair * HALF:(pair + 1) * HALF, :].rearrange("(n p) v -> p n v", p=P), result[:])
+        result = keep.tile([P, 2, P], F32, name="result_pair")
+        nc.vector.tensor_copy(out=result[:, 1, :], in_=finals[1][:])
+        nc.scalar.copy(out=result[:, 0, :], in_=finals[0][:])
+        nc.sync.dma_start(out[0:HALF, :].rearrange("(n p) v -> p n v", p=P), result[:])
+        result = keep.tile([P, P], F32, name="result_third")
+        nc.scalar.copy(out=result[:], in_=finals[2][:])
+        nc.sync.dma_start(out[HALF:LAST * P, :], result[:])
+        result = keep.tile([P, P], F32, name="result_last")
+        nc.vector.tensor_copy(out=result[:], in_=finals[LAST][:])
+        nc.sync.dma_start(out[LAST * P:V, :], result[:])

@@ -25,7 +25,7 @@ RUNS = S // D
 HALF = V // 2
 BAND_BYTES = S * 4
 GROUPED_BYTES = P * PACK * 2
-HEAD = T // 2
+HEAD = T // 4
 
 
 def tile_picked_ydice_dice_p_kernel(tc, x_words, x_scales, hT, goal, offs, out):
@@ -38,23 +38,22 @@ def tile_picked_ydice_dice_p_kernel(tc, x_words, x_scales, hT, goal, offs, out):
         psum = ctx.enter_context(tc.psum_pool(name="psum", bufs=1))
 
         offsets = keep.tile([P, S // 16], U16, name="offsets")
-        table_scales = early.tile([P, PASSES, T], U8, name="table_scales", offset=2 * BAND_BYTES - 32)
+        table_scales = early.tile([P, T], U8, name="table_scales", offset=2 * BAND_BYTES - 32)
         table_words = [reuse.tile([P, T], U32, name="table_words0", offset=2 * BAND_BYTES - 32),
-                       keep.tile([P, T], U32, name="table_words1")]
+                       early.tile([P, T], U32, name="table_words1", offset=3 * BAND_BYTES - 64)]
         h_first = keep.tile([P, PACK, V], F32, name="h_first")
         h_second = [early.tile([P, PACK, HALF], F32, name="h_second0", offset=0),
                     reuse.tile([P, PACK, P], F32, name="h_second2", offset=BAND_BYTES),
                     reuse.tile([P, PACK, P], F32, name="h_second3", offset=2 * BAND_BYTES)]
         goal_sb = [reuse.tile([P, S], F32, name="goal%d" % b, offset=(3 + b) * BAND_BYTES) for b in range(LAST)]
-        goal_sb.append(early.tile([P, S], F32, name="goal%d" % LAST, offset=4 * BAND_BYTES))
+        goal_sb.append(early.tile([P, S], F32, name="goal%d" % LAST, offset=8 * BAND_BYTES))
         ident = keep.tile([P, P], F32, name="ident")
-        picked_scales = early.tile([P, PASSES, S], U8, name="picked_scales", offset=4 * BAND_BYTES)
-        x_scale_rows = keep.tile([P, PASSES, S], U8, name="x_scale_rows", align_bytes=64)
+        picked_scales = early.tile([P, S], U8, name="picked_scales", offset=8 * BAND_BYTES)
+        x_scale_rows = [keep.tile([P, S], U8, name="x_scale_rows%d" % o, align_bytes=64) for o in range(PASSES)]
         x_codes = [keep.tile([P, S], U32, name="x_codes%d" % o, align_bytes=64) for o in range(PASSES)]
-        table_words_view = table_scales[:].rearrange("p o c -> p (o c)").bitcast(I32)
-        nc.gpsimd.memset(table_words_view[:, 0:768], 0)
-        nc.vector.memset(table_words_view[:, 768:1024], 0)
-        nc.vector.memset(x_scale_rows[:].rearrange("p o c -> p (o c)").bitcast(I32), 0)
+        nc.gpsimd.memset(table_scales[:].bitcast(I32), 0)
+        for o in range(PASSES):
+            nc.vector.memset(x_scale_rows[o][:].bitcast(I32), 0)
 
         zero = late.tile([P, 1], F32, name="zero", offset=LAST * BAND_BYTES)
         half = keep.tile([P, 1], F32, name="half")
@@ -67,20 +66,25 @@ def tile_picked_ydice_dice_p_kernel(tc, x_words, x_scales, hT, goal, offs, out):
 
         load_words(0, 0, HEAD)
         nc.sync.dma_start(offsets[:], offs)
-        nc.sync.dma_start(table_scales[0:P:8, :, :].bitcast(I32), x_scales.rearrange("o q c -> q o c").bitcast(I32))
+        nc.sync.dma_start(table_scales[0:P:4, :].bitcast(I32), x_scales.rearrange("o q c -> (o q) c").bitcast(I32))
         load_words(0, HEAD, T)
         make_identity(nc, ident[:])
         nc.sync.dma_start(h_first[:], hT[0:PACK * P, :].rearrange("(p j) t -> p j t", j=PACK))
+        nc.vector.tensor_copy(picked_scales[:], table_scales[:].indirect(offsets[:]))
+
+        def move_scale_rows(o):
+            for r in range(4):
+                nc.sync.dma_start(x_scale_rows[o][r:P:32, :].bitcast(I32),
+                                  picked_scales[64 * o + 4 * r:64 * (o + 1):16, :].bitcast(I32))
+
+        move_scale_rows(0)
         load_words(1, 0, T)
-        for o in range(PASSES):
-            nc.vector.tensor_copy(picked_scales[:, o, :], table_scales[:, o, :].indirect(offsets[:]))
-        for r in range(4):
-            nc.sync.dma_start(x_scale_rows[r:P:32, :, :].rearrange("p o c -> p (o c)").bitcast(I32),
-                              picked_scales[8 * r:P:32, :, :].rearrange("p o c -> p (o c)").bitcast(I32))
         nc.vector.tensor_copy(x_codes[0][:], table_words[0][:].indirect(offsets[:]))
         for piece, (first, last) in zip(h_second, ((0, HALF), (HALF, LAST * P), (LAST * P, V))):
             rows = hT[PACK * P:2 * PACK * P, first:last]
             nc.sync.dma_start(piece[:], rows.rearrange("(p j) t -> p j t", j=PACK))
+            if first == 0:
+                move_scale_rows(1)
         for b in range(BANDS):
             nc.sync.dma_start(goal_sb[b][:], goal[b * P:(b + 1) * P, :])
 
@@ -117,7 +121,7 @@ def tile_picked_ydice_dice_p_kernel(tc, x_words, x_scales, hT, goal, offs, out):
         def product(o, b, opens):
             nc.tensor.matmul_mx(out=scores[b][:], lhsT=h_codes[o][b][:].bitcast(FP8X4),
                                 lhsT_scale=h_scale_rows[o][b][:], rhs=x_codes[o][:].bitcast(FP8X4),
-                                rhs_scale=x_scale_rows[:, o, :], start=opens, stop=not opens)
+                                rhs_scale=x_scale_rows[o][:], start=opens, stop=not opens)
 
         for b in range(BANDS):
             prepare(0, b, b % 2 == 0)
@@ -175,7 +179,7 @@ def tile_picked_ydice_dice_p_kernel(tc, x_words, x_scales, hT, goal, offs, out):
 
         def warm_up(unread):
             nc.tensor.matmul_mx(out=unread, lhsT=h_codes[0][0][:].bitcast(FP8X4), lhsT_scale=h_scale_rows[0][0][:],
-                                rhs=x_codes[0][:, 0:HALF].bitcast(FP8X4), rhs_scale=x_scale_rows[:, 0, 0:HALF],
+                                rhs=x_codes[0][:, 0:HALF].bitcast(FP8X4), rhs_scale=x_scale_rows[0][:, 0:HALF],
                                 start=True, stop=True)
 
         for b in range(2):

@@ -125,13 +125,15 @@ def tile_picked_ydice_dice_p_kernel(tc, x_words, x_scales, hT, goal, offs, out):
 
         for b in range(BANDS):
             prepare(0, b, b % 2 == 0)
-        for b in range(LAST):
+        for b in range(BANDS):
             product(0, b, True)
         nc.vector.tensor_copy(x_codes[1][:], table_words[1][:].indirect(offsets[:]))
         for b in range(BANDS):
             prepare(1, b, b != 1)
-            product(1, b, b == LAST)
-        product(0, LAST, False)
+            product(1, b, False)
+        unread = psum.tile([P, S], F32, name="unread", tag="spare")
+        nc.tensor.matmul_mx(out=unread[:], lhsT=h_codes[1][LAST][:].bitcast(FP8X4), lhsT_scale=h_scale_rows[1][LAST][:],
+                            rhs=x_codes[1][:].bitcast(FP8X4), rhs_scale=x_scale_rows[1][:], start=True, stop=True)
 
         def turned_sum(acc, parts, opens=True, closes=True):
             for n, part in enumerate(parts):
@@ -187,8 +189,7 @@ def tile_picked_ydice_dice_p_kernel(tc, x_words, x_scales, hT, goal, offs, out):
             make_shifted(b)
         for b in range(2, BANDS):
             make_overlap(b)
-            for repeat in range(2):
-                warm_up(sum_overlap[1][:, HALF:V])
+            warm_up(sum_overlap[1][:, HALF:V])
         for b in range(2, BANDS):
             make_shifted(b)
 

@@ -55,7 +55,7 @@ def tile_picked_ydice_dice_p_kernel(tc, x_words, x_scales, hT, goal, offs, out):
         for o in range(PASSES):
             nc.vector.memset(x_scale_rows[o][:].bitcast(I32), 0)
 
-        zero = late.tile([P, 1], F32, name="zero", offset=LAST * BAND_BYTES)
+        zero = keep.tile([P, 1], F32, name="zero")
         half = keep.tile([P, 1], F32, name="half")
         nc.vector.memset(zero[:], 0.0)
         nc.scalar.activation(out=half[:], in_=zero[:], func=ACT.Sigmoid)
@@ -174,10 +174,10 @@ def tile_picked_ydice_dice_p_kernel(tc, x_words, x_scales, hT, goal, offs, out):
 
         def make_shifted(b):
             with_goal(missing[b], b, ALU.subtract)
-            if b >= 1:
-                turned_missing[b] = psum.tile([P, D, P], F32, name="turned_missing%d" % b, tag=("band1", "spare", "band3")[b - 1])
-                for d in range(D):
-                    nc.tensor.transpose(turned_missing[b][:, d, :], missing[b][:, d, :], ident[:])
+            turned_missing[b] = psum.tile([P, D, P], F32, name="turned_missing%d" % b,
+                                          tag=("band0", "band1", "spare", "band3")[b])
+            for d in range(D):
+                nc.tensor.transpose(turned_missing[b][:, d, :], missing[b][:, d, :], ident[:])
 
         def warm_up(unread):
             nc.tensor.matmul_mx(out=unread, lhsT=h_codes[0][0][:].bitcast(FP8X4), lhsT_scale=h_scale_rows[0][0][:],
@@ -194,12 +194,10 @@ def tile_picked_ydice_dice_p_kernel(tc, x_words, x_scales, hT, goal, offs, out):
             make_shifted(b)
 
         root = keep.tile([P, V], F32, name="root")
-        six = late.tile([P, LAST * S], F32, name="six", offset=0)
+        six = late.tile([P, BANDS * S], F32, name="six", offset=0)
         nc.gpsimd.memset(six[:, 0:1], 4.0)
         nc.scalar.activation(out=root[:], in_=sum_score[:], func=ACT.Abs_reciprocal_sqrt, bias=six[:, 0:1])
-        squares = [late.tile([P, D, RUNS], F32, name="squares0", offset=LAST * BAND_BYTES)]
-        squares.extend(late.tile([P, D, RUNS], F32, name="squares%d" % b, offset=(b - 1) * BAND_BYTES)
-                       for b in range(1, BANDS))
+        squares = [late.tile([P, D, RUNS], F32, name="squares%d" % b, offset=b * BAND_BYTES) for b in range(BANDS)]
         half_ratio = keep.tile([P, V], F32, name="half_ratio")
         minus_ratio = keep.tile([P, V], F32, name="minus_ratio")
 
@@ -218,30 +216,23 @@ def tile_picked_ydice_dice_p_kernel(tc, x_words, x_scales, hT, goal, offs, out):
         make_minus_ratio(0)
         make_minus_ratio(1)
 
-        sum_first = psum.tile([P, P], F32, name="sum_first", tag="band0")
-        nc.scalar.activation(out=squares[0][:], in_=missing[0][:], func=ACT.Square)
-        turned_sum(sum_first[:], [squares[0][:, d, :] for d in range(D)])
-        loss = keep.tile([P, P], F32, name="loss")
-        nc.vector.scalar_tensor_tensor(out=loss[:], in0=sum_first[:], scalar=1.0 / D, in1=minus_ratio[:, 0:P],
-                                       op0=ALU.mult, op1=ALU.add)
-        finals = [psum.tile([P, P], F32, name="final0", tag="final0")]
-        for b, bank in ((1, "band2"), (2, "sum_overlap0"), (3, "sum_overlap1")):
-            nc.scalar.activation(out=squares[b][:], in_=turned_missing[b][:], func=ACT.Square,
-                                 scale=half[:, 0:1])
-            finals.append(psum.tile([P, P], F32, name="final%d" % b, tag=bank))
+        final_pair = psum.tile([P, 2, P], F32, name="final_pair", tag="final_pair")
+        finals = [final_pair[:, 0, :], final_pair[:, 1, :],
+                  psum.tile([P, P], F32, name="final2", tag="band2")[:],
+                  psum.tile([P, P], F32, name="final3", tag="band0")[:]]
+        for b in range(BANDS):
+            nc.scalar.activation(out=squares[b][:], in_=turned_missing[b][:], func=ACT.Square, scale=half[:, 0:1])
             if b < LAST:
-                turned_sum(finals[b][:], planes(squares[b]), closes=False)
-        turned_sum(finals[1][:], [minus_ratio[:, P:HALF]], opens=False)
-        turned_sum(finals[2][:], [minus_ratio[:, HALF:LAST * P]], opens=False)
-        nc.tensor.transpose(finals[0][:], loss[:], ident[:])
-        turned_sum(finals[LAST][:], [minus_ratio[:, LAST * P:V]] + planes(squares[LAST]))
+                turned_sum(finals[b], planes(squares[b]), opens=(b != 1), closes=False)
+        for b in range(LAST):
+            turned_sum(finals[b], [minus_ratio[:, b * P:(b + 1) * P]], opens=False, closes=(b != 0))
+        turned_sum(finals[LAST], [minus_ratio[:, LAST * P:V]] + planes(squares[LAST]))
         result = keep.tile([P, 2, P], F32, name="result_pair")
-        nc.vector.tensor_copy(out=result[:, 1, :], in_=finals[1][:])
-        nc.scalar.copy(out=result[:, 0, :], in_=finals[0][:])
+        nc.scalar.copy(out=result[:], in_=final_pair[:])
         nc.sync.dma_start(out[0:HALF, :].rearrange("(n p) v -> p n v", p=P), result[:])
         result = keep.tile([P, P], F32, name="result_third")
-        nc.scalar.copy(out=result[:], in_=finals[2][:])
+        nc.vector.tensor_copy(out=result[:], in_=finals[2])
         nc.sync.dma_start(out[HALF:LAST * P, :], result[:])
         result = keep.tile([P, P], F32, name="result_last")
-        nc.vector.tensor_copy(out=result[:], in_=finals[LAST][:])
+        nc.vector.tensor_copy(out=result[:], in_=finals[LAST])
         nc.sync.dma_start(out[LAST * P:V, :], result[:])

from contextlib import ExitStack

import concourse.mybir as mybir
from concourse.masks import make_identity

K, T, S, V, D = 1024, 2048, 512, 512, 4
FLOPS = 2 * K * S * V

F32 = mybir.dt.float32
BF16 = mybir.dt.bfloat16
I32 = mybir.dt.int32
U32 = mybir.dt.uint32
U16 = mybir.dt.uint16
U8 = mybir.dt.uint8
FP8X4 = mybir.dt.float8_e4m3fn_x4
ACT = mybir.ActivationFunctionType
ALU = mybir.AluOpType

P = 128
PACK = 4
PASSES = K // (PACK * P)
BANDS = V // P
LAST = BANDS - 1
RUNS = S // D
HALF = V // 2
BAND_BYTES = S * 4
GROUPED_BYTES = P * PACK * 2
HEAD = T // 4


def tile_picked_ydice_dice_p_kernel(tc, x_words, x_scales, hT, goal, offs, out):
    nc = tc.nc
    with ExitStack() as ctx:
        keep = ctx.enter_context(tc.tile_pool(name="keep", bufs=1))
        late = ctx.enter_context(tc.tile_pool(name="late", bufs=1))
        reuse = ctx.enter_context(tc.tile_pool(name="reuse", bufs=1))
        early = ctx.enter_context(tc.tile_pool(name="early", bufs=1))
        psum = ctx.enter_context(tc.psum_pool(name="psum", bufs=1))

        offsets = keep.tile([P, S // 16], U16, name="offsets")
        table_scales = early.tile([P, T], U8, name="table_scales", offset=2 * BAND_BYTES - 32)
        table_words = [reuse.tile([P, T], U32, name="table_words0", offset=2 * BAND_BYTES - 32),
                       early.tile([P, T], U32, name="table_words1", offset=3 * BAND_BYTES - 64)]
        h_first = keep.tile([P, PACK, V], F32, name="h_first")
        h_second = [early.tile([P, PACK, HALF], F32, name="h_second0", offset=0),
                    reuse.tile([P, PACK, P], F32, name="h_second2", offset=BAND_BYTES),
                    reuse.tile([P, PACK, P], F32, name="h_second3", offset=2 * BAND_BYTES)]
        goal_sb = [reuse.tile([P, S], F32, name="goal%d" % b, offset=(3 + b) * BAND_BYTES) for b in range(LAST)]
        goal_sb.append(early.tile([P, S], F32, name="goal%d" % LAST, offset=8 * BAND_BYTES))
        ident = keep.tile([P, P], F32, name="ident")
        picked_scales = early.tile([P, S], U8, name="picked_scales", offset=8 * BAND_BYTES)
        x_scale_rows = [keep.tile([P, S], U8, name="x_scale_rows%d" % o, align_bytes=64) for o in range(PASSES)]
        x_codes = [keep.tile([P, S], U32, name="x_codes%d" % o, align_bytes=64) for o in range(PASSES)]
        nc.gpsimd.memset(table_scales[:].bitcast(I32), 0)
        for o in range(PASSES):
            nc.vector.memset(x_scale_rows[o][:].bitcast(I32), 0)

        zero = keep.tile([P, 1], F32, name="zero")
        half = keep.tile([P, 1], F32, name="half")
        nc.vector.memset(zero[:], 0.0)
        nc.scalar.activation(out=half[:], in_=zero[:], func=ACT.Sigmoid)

        def load_words(o, first, last):
            words = x_words[o].rearrange("p c r -> p (c r)").bitcast(I32)
            nc.sync.dma_start(table_words[o][:, first:last].bitcast(I32), words[:, first:last])

        load_words(0, 0, HEAD)
        nc.sync.dma_start(offsets[:], offs)
        nc.sync.dma_start(table_scales[0:P:4, :].bitcast(I32), x_scales.rearrange("o q c -> (o q) c").bitcast(I32))
        load_words(0, HEAD, T)
        make_identity(nc, ident[:])
        nc.sync.dma_start(h_first[:], hT[0:PACK * P, :].rearrange("(p j) t -> p j t", j=PACK))
        nc.vector.tensor_copy(picked_scales[:], table_scales[:].indirect(offsets[:]))

        def move_scale_rows(o):
            for r in range(4):
                nc.sync.dma_start(x_scale_rows[o][r:P:32, :].bitcast(I32),
                                  picked_scales[64 * o + 4 * r:64 * (o + 1):16, :].bitcast(I32))

        move_scale_rows(0)
        load_words(1, 0, T)
        nc.vector.tensor_copy(x_codes[0][:], table_words[0][:].indirect(offsets[:]))
        for piece, (first, last) in zip(h_second, ((0, HALF), (HALF, LAST * P), (LAST * P, V))):
            rows = hT[PACK * P:2 * PACK * P, first:last]
            nc.sync.dma_start(piece[:], rows.rearrange("(p j) t -> p j t", j=PACK))
            if first == 0:
                move_scale_rows(1)
        for b in range(BANDS):
            nc.sync.dma_start(goal_sb[b][:], goal[b * P:(b + 1) * P, :])

        def grouped_tile(o, b):
            name = "grouped%d_%d" % (o, b)
            if (o, b) == (PASSES - 1, LAST):
                return reuse.tile([P, P, PACK], BF16, name=name, align_bytes=64,
                                  offset=7 * BAND_BYTES - GROUPED_BYTES // 2)
            return keep.tile([P, P, PACK], BF16, name=name, align_bytes=64)

        grouped = [[grouped_tile(o, b) for b in range(BANDS)] for o in range(PASSES)]
        h_codes = [[keep.tile([P, P], U32, name="h_codes%d_%d" % (o, b), align_bytes=64)
                    for b in range(BANDS)] for o in range(PASSES)]
        h_scale_rows = [[keep.tile([P, P], U8, name="h_scale_rows%d_%d" % (o, b), align_bytes=64)
                         for b in range(BANDS)] for o in range(PASSES)]
        scores = [psum.tile([P, S], F32, name="scores%d" % b, tag="band%d" % b) for b in range(BANDS)]

        def raw_band(o, b):
            if o == 0:
                return h_first[:, :, b * P:(b + 1) * P]
            if b < 2:
                return h_second[0][:, :, b * P:(b + 1) * P]
            return h_second[b - 1][:]

        def prepare(o, b, on_vector):
            if on_vector:
                nc.vector.tensor_copy(out=grouped[o][b][:].rearrange("p (c i) j -> p c j i", i=4),
                                      in_=raw_band(o, b).rearrange("p j (c i) -> p c j i", i=4))
            else:
                nc.scalar.copy(out=grouped[o][b][:], in_=raw_band(o, b).rearrange("p j t -> p t j"))
            nc.vector.quantize_mx(out=h_codes[o][b][:].bitcast(FP8X4), scales=h_scale_rows[o][b][:],
                                  in_=grouped[o][b][:].rearrange("p t j -> p (t j)"))

        def product(o, b, opens):
            nc.tensor.matmul_mx(out=scores[b][:], lhsT=h_codes[o][b][:].bitcast(FP8X4),
                                lhsT_scale=h_scale_rows[o][b][:], rhs=x_codes[o][:].bitcast(FP8X4),
                                rhs_scale=x_scale_rows[o][:], start=opens, stop=not opens)

        for b in range(BANDS):
            prepare(0, b, b % 2 == 0)
        for b in range(BANDS):
            product(0, b, True)
        nc.vector.tensor_copy(x_codes[1][:], table_words[1][:].indirect(offsets[:]))
        for b in range(BANDS):
            prepare(1, b, b != 1)
            product(1, b, False)
        unread = psum.tile([P, S], F32, name="unread", tag="spare")
        nc.tensor.matmul_mx(out=unread[:], lhsT=h_codes[1][LAST][:].bitcast(FP8X4), lhsT_scale=h_scale_rows[1][LAST][:],
                            rhs=x_codes[1][:].bitcast(FP8X4), rhs_scale=x_scale_rows[1][:], start=True, stop=True)

        def turned_sum(acc, parts, opens=True, closes=True):
            for n, part in enumerate(parts):
                nc.tensor.matmul(out=acc, lhsT=part, rhs=ident[:], is_transpose=True,
                                 start=(opens and n == 0), stop=(closes and n == len(parts) - 1))

        def band_tile(name, b, shape, reused):
            if b in reused:
                return reuse.tile(shape, F32, name="%s%d" % (name, b), offset=reused[b] * BAND_BYTES)
            return keep.tile(shape, F32, name="%s%d" % (name, b))

        score = [band_tile("score", b, [P, D, RUNS], {}) for b in range(BANDS)]
        overlap = [band_tile("overlap", b, [P, D, RUNS], {0: 6}) for b in range(BANDS)]
        missing = [band_tile("missing", b, [P, D, RUNS], {0: 7}) for b in range(BANDS)]
        sum_score = psum.tile([P, V], F32, name="sum_score", tag="band2")
        sum_overlap = [psum.tile([P, (pair + 1) * HALF], F32, name="sum_overlap%d" % pair, tag="sum_overlap%d" % pair)
                       for pair in range(2)]

        def planes(tile):
            return [tile[:, d, :] for d in range(D)]

        for b in range(BANDS):
            nc.scalar.activation(out=score[b][:], in_=scores[b][:].rearrange("p (v d) -> p d v", d=D),
                                 func=ACT.Sigmoid, bias=zero[:])
        for b in range(BANDS):
            turned_sum(sum_score[:, b * P:(b + 1) * P], planes(score[b]))

        def with_goal(result, b, op):
            walk = "p d (c i) -> p c d i"
            nc.vector.tensor_tensor(out=result[:].rearrange(walk, i=2), in0=score[b][:].rearrange(walk, i=2),
                                    in1=goal_sb[b][:].rearrange("p (c i d) -> p c d i", i=2, d=D), op=op)

        def make_overlap(b):
            with_goal(overlap[b], b, ALU.mult)
            turned_sum(sum_overlap[b // 2][:, (b % 2) * P:(b % 2 + 1) * P], planes(overlap[b]))

        turned_missing = {}

        def make_shifted(b):
            with_goal(missing[b], b, ALU.subtract)
            turned_missing[b] = psum.tile([P, D, P], F32, name="turned_missing%d" % b,
                                          tag=("band0", "band1", "spare", "band3")[b])
            for d in range(D):
                nc.tensor.transpose(turned_missing[b][:, d, :], missing[b][:, d, :], ident[:])

        def warm_up(unread):
            nc.tensor.matmul_mx(out=unread, lhsT=h_codes[0][0][:].bitcast(FP8X4), lhsT_scale=h_scale_rows[0][0][:],
                                rhs=x_codes[0][:, 0:HALF].bitcast(FP8X4), rhs_scale=x_scale_rows[0][:, 0:HALF],
                                start=True, stop=True)

        for b in range(2):
            make_overlap(b)
            make_shifted(b)
        for b in range(2, BANDS):
            make_overlap(b)
            warm_up(sum_overlap[1][:, HALF:V])
        for b in range(2, BANDS):
            make_shifted(b)

        root = keep.tile([P, V], F32, name="root")
        six = late.tile([P, BANDS * S], F32, name="six", offset=0)
        nc.gpsimd.memset(six[:, 0:1], 4.0)
        nc.scalar.activation(out=root[:], in_=sum_score[:], func=ACT.Abs_reciprocal_sqrt, bias=six[:, 0:1])
        squares = [late.tile([P, D, RUNS], F32, name="squares%d" % b, offset=b * BAND_BYTES) for b in range(BANDS)]
        half_ratio = keep.tile([P, V], F32, name="half_ratio")
        minus_ratio = keep.tile([P, V], F32, name="minus_ratio")

        def make_half_ratio(pair):
            cols = slice(pair * HALF, (pair + 1) * HALF)
            nc.vector.scalar_tensor_tensor(out=half_ratio[:, cols], in0=sum_overlap[pair][:, 0:HALF], scalar=0.5,
                                           in1=root[:, cols], op0=ALU.add, op1=ALU.mult)

        def make_minus_ratio(pair):
            cols = slice(pair * HALF, (pair + 1) * HALF)
            nc.vector.scalar_tensor_tensor(out=minus_ratio[:, cols], in0=half_ratio[:, cols], scalar=-2.0,
                                           in1=root[:, cols], op0=ALU.mult, op1=ALU.mult)

        make_half_ratio(0)
        make_half_ratio(1)
        make_minus_ratio(0)
        make_minus_ratio(1)

        final_pair = psum.tile([P, 2, P], F32, name="final_pair", tag="final_pair")
        finals = [final_pair[:, 0, :], final_pair[:, 1, :],
                  psum.tile([P, P], F32, name="final2", tag="band2")[:],
                  psum.tile([P, P], F32, name="final3", tag="band0")[:]]
        for b in range(BANDS):
            nc.scalar.activation(out=squares[b][:], in_=turned_missing[b][:], func=ACT.Square, scale=half[:, 0:1])
            if b < LAST:
                turned_sum(finals[b], planes(squares[b]), opens=(b != 1), closes=False)
        for b in range(LAST):
            turned_sum(finals[b], [minus_ratio[:, b * P:(b + 1) * P]], opens=False, closes=(b != 0))
        turned_sum(finals[LAST], [minus_ratio[:, LAST * P:V]] + planes(squares[LAST]))
        result = keep.tile([P, 2, P], F32, name="result_pair")
        nc.scalar.copy(out=result[:], in_=final_pair[:])
        nc.sync.dma_start(out[0:HALF, :].rearrange("(n p) v -> p n v", p=P), result[:])
        result = keep.tile([P, P], F32, name="result_third")
        nc.vector.tensor_copy(out=result[:], in_=finals[2])
        nc.sync.dma_start(out[HALF:LAST * P, :], result[:])
        result = keep.tile([P, P], F32, name="result_last")
        nc.vector.tensor_copy(out=result[:], in_=finals[LAST])
        nc.sync.dma_start(out[LAST * P:V, :], result[:])
